import numpy as np
CORES = [242,247,114,119]
N = 4
T, FF, CAPT = 2048, 32, 2048
def entries(a): return a.T.reshape(-1)
def pack(v, P): return np.ascontiguousarray(np.asarray(v, np.int32).reshape(-1, P).T)
def lists(rng, how):
    w = rng.random(N) ** 2 + 1e-3; c = T // 8 + ((CAPT - N * (T // 8)) * w / w.sum()).astype(np.int64)
    a = rng.permutation(N)
    if how == "few": c = np.zeros(N, np.int64); c[N - 1] = 3; c[int(rng.integers(N - 1))] = 1
    if how == "lone": s = int(rng.integers(CAPT - T + 1)); c = np.zeros(N, np.int64); c[a[0]] = T; c[a[1]] = s; c[a[2]] = CAPT - T - s
    if how == "none": c = np.zeros(N, np.int64)
    if how == "pair": s = 2 * int(rng.integers(512, 767)) + 1; c = np.zeros(N, np.int64); c[a[0]] = s; c[a[1]] = CAPT - s - 1; c[a[2]] = 1
    if how == "zeros": c = np.full(N, 2); c[0] = T - 7 - 2 * int(rng.integers(T // 16))
    K = np.stack([rng.permutation(np.arange(T) < c[r]) for r in range(N)])
    if how == "zeros": K = np.stack([np.r_[True, rng.permutation(np.arange(T - 2) < c[r] - 2), True] for r in range(N)])
    return {"keep": np.stack([pack(k, 16) for k in K])}
def blank(d):
    for r in range(N):
        k = entries(d["keep"][r]); d["x"][r][:, np.nonzero(k)[0][1:-1:4]] = 0; d["x"][r][:, np.nonzero(1 - k)[0][::4]] = 0
def setup_inputs(rng):
    return dict({"x": rng.standard_normal((N, 128, T), dtype=np.float32), "w1": np.repeat((rng.standard_normal((1, 128, FF * 128), dtype=np.float32) / 8), N, axis=0), "w2": np.repeat((rng.standard_normal((1, 128, FF * 128), dtype=np.float32) / 64), N, axis=0)}, **lists(rng, "uniform"))
def setup_inputs_few(rng):
    d = setup_inputs(rng); d.update(lists(rng, "few"))
    for k in ("x",): d[k] = (d[k].astype(np.float32) * 1024.0).astype(d[k].dtype)
    return d
def setup_inputs_lone(rng):
    d = setup_inputs(rng); d.update(lists(rng, "lone"))
    for k in ("x",): d[k] = (d[k].astype(np.float32) * (1 / 1024.0)).astype(d[k].dtype)
    return d
def setup_inputs_none(rng):
    d = setup_inputs(rng); d.update(lists(rng, "none"))
    return d
def setup_inputs_pair(rng):
    d = setup_inputs(rng); d.update(lists(rng, "pair"))
    return d
def setup_inputs_zeros(rng):
    d = setup_inputs(rng); d.update(lists(rng, "zeros"))
    blank(d)
    return d
def check_inputs(x):
    bad = []
    if x["keep"].min() < 0 or x["keep"].max() >= 2: bad.append("keep out of range")
    if int(x["keep"].sum()) > CAPT: bad.append("more than CAPT tokens are kept in all")
    if any((x[k] != x[k][:1]).any() for k in ("w1", "w2")): bad.append("w1 or w2 is not alike on all ranks")
    return bad
def reference(x, w1, w2, keep):
    X, W1, W2 = x.astype(np.float64), w1.astype(np.float64), w2.astype(np.float64)
    Y = X.copy()
    for r in range(N):
        P = np.nonzero(entries(keep[r]) == 1)[0]
        if len(P) == 0: continue
        Y[r][:, P] = sum(W2[r][:, 128 * f:128 * f + 128].T @ np.maximum(W1[r][:, 128 * f:128 * f + 128].T @ X[r][:, P], 0.0) for f in range(FF))
    return {"y": Y.astype(np.float32)}

@@ -1,0 +1,340 @@
+from concourse.bass import DstId, RemoteDMATransfer
+from concourse.mybir import AluOpType, AxisListType, ActivationFunctionType
+
+NF = 16
+PIECES = 4
+NH = 5
+NR = 5
+LOOK = 2
+SLW = 2048 + 368
+RES = 2052
+
+SCRATCH = {
+    "k8": ("sbuf", [128, 16], "int32"), "k8b": ("sbuf", [128, 16], "bfloat16"), "k8n": ("sbuf", [128, 16], "bfloat16"),
+    "ki": ("sbuf", [128, 128], "int32"), "kib": ("sbuf", [128, 128], "bfloat16"), "kin": ("sbuf", [128, 128], "bfloat16"),
+    "ones": ("sbuf", [128, 128], "bfloat16"), "onef": ("sbuf", [128, 128], "float32"),
+    "mu": ("sbuf", [128, 128], "bfloat16"), "me": ("sbuf", [128, 128], "bfloat16"), "mb": ("sbuf", [128, 128], "bfloat16"),
+    "r1": ("sbuf", [128, 128], "bfloat16"), "ut": ("sbuf", [128, 128], "bfloat16"),
+    "ii": ("sbuf", [128, 4], "int32"),
+    "ff": ("sbuf", [128, 8], "float32"),
+    "q": ("sbuf", [128, 144], "bfloat16"), "val0": ("sbuf", [128, 256], "bfloat16"), "val": ("sbuf", [128, 256], "bfloat16"),
+    "ts": ("sbuf", [128, 112], "float32"),
+    "off": ("sbuf", [128, 16], "uint16"),
+    "sl": ("sbuf", [128, SLW], "bfloat16"), "lo": ("sbuf", [128, 128], "uint16"), "ro": ("sbuf", [128, 128], "uint16"),
+    "rr": ("sbuf", [128, 1152], "float32"), "ri": ("sbuf", [128, 384], "int32"),
+    "xr": ("sbuf", [128, 4100], "float32"), "pk": ("sbuf", [128, 2048], "float32"), "yt": ("sbuf", [128, 2048], "float32"),
+    "wa": ("sbuf", [128, 2048], "float32"), "wb": ("sbuf", [128, 2048], "float32"),
+    "tk0": ("sbuf", [128, 256], "float32"), "tk1": ("sbuf", [128, 256], "float32"),
+    "xx": ("sbuf", [128, 512], "float32"),
+    "yo": ("sbuf", [128, 256], "float32"), "yp": ("sbuf", [128, 256], "float32"), "ys": ("sbuf", [128, 256], "float32"),
+    "yb0": ("psum", [128, 512], "float32"), "yb1": ("psum", [128, 512], "float32"), "lb": ("psum", [128, 512], "float32"),
+}
+for _i in range(NH):
+    SCRATCH["hb%d" % _i] = ("psum", [128, 512], "float32")
+for _i in range(NR):
+    SCRATCH["hr%d" % _i] = ("sbuf", [128, 512], "float32")
+SEMAPHORES = ["c_pe", "c_v", "c_s", "c_g", "d_k8", "d_x", "d_ki", "d_st", "snd", "tk0", "tk1", "xf", "yp", "res"] + \
+    ["w%d" % k for k in range(PIECES)]
+
+
+def rank_program(g, core, T, topo):
+    def place(c):
+        return (topo.host(c), topo.chip(c))
+
+    ranks = [c for c in T.cores if place(c) == place(core)]
+    if not ranks:
+        return
+    mine = [c for c in range(256) if place(c) == place(core)]
+    dies = [[r] + [c for c in mine if topo.die(c) == topo.die(r) and c != r] for r in ranks]
+    d = [i for i in range(2) if core in dies[i]][0]
+    w = dies[d].index(core)
+    is_rank = w == 0
+    partner = dies[1 - d][w]
+
+    add, sub, mult = AluOpType.add, AluOpType.subtract, AluOpType.mult
+    Copy, Relu = ActivationFunctionType.Copy, ActivationFunctionType.Relu
+    V, S, PE = g.vector, g.scalar, g.tensor
+    queues = {"pe": g.tensor, "v": g.vector, "s": g.scalar, "g": g, "sy": g.sync}
+    total, waited, seen = {}, {}, {}
+
+    def need(qn, *deps):
+        best = {}
+        for dep in deps:
+            if dep is not None:
+                best[dep[0]] = max(best.get(dep[0], 0), dep[1])
+        for s, v in best.items():
+            if waited.get((qn, s), 0) < v:
+                queues[qn].wait_ge(T.sem[s], v)
+                waited[(qn, s)] = v
+                seen[s] = max(seen.get(s, 0), v)
+
+    def expect(s, n):
+        total[s] = total.get(s, 0) + n
+        return (s, total[s])
+
+    def done(qn, inst):
+        inst.then_inc(T.sem["c_" + qn], 1)
+        return expect("c_" + qn, 1)
+
+    def dma(inst, s):
+        inst.then_inc(T.sem[s], 16)
+        return expect(s, 16)
+
+    def parts(n, dsts):
+        m = topo.mask(core, dsts[0])
+        for c in dsts:
+            m &= topo.mask(core, c)
+        bits = [1 << i for i in range(16) if (m >> i) & 1]
+        k = len(bits) // n
+        return [sum(bits[i * k:(i + 1) * k]) for i in range(n)], k
+
+    def ids(dsts):
+        out = []
+        for c in dsts:
+            rid, pid = topo.addr(c, core)
+            out.append(DstId(rid=rid, pnc=pid))
+        return out
+
+    def send(items, n):
+        tr = []
+        for j, (dsts, src, dst, s) in enumerate(items):
+            ms, k = parts(n, dsts)
+            tr.append(RemoteDMATransfer(dst_ids=ids(dsts), srcs=[src], dsts=[dst for _ in dsts],
+                                        dma_engine_mask=ms[j], remote_sem=T.sem[s]))
+            expect("snd", k)
+        g.remote_dma_fused(tr, local_sem=T.sem["snd"])
+
+    def send_piece(k, dsts):
+        c = slice(512 * k, 512 * k + 512)
+        send([(dsts, T.wa[:, c], T.wa[:, c], "w%d" % k), (dsts, T.wb[:, c], T.wb[:, c], "w%d" % k)], 2)
+
+    relay = [1 + k % 3 for k in range(PIECES)]
+    piece = [None] * PIECES
+
+    def pass_on(k):
+        if not is_rank and w == relay[k]:
+            need("g", piece[k])
+            send_piece(k, [dies[d][j] for j in (1, 2, 3) if j != w])
+
+    lists = {}
+    hb_free = [None] * NH
+    ge = AluOpType.is_ge
+    if is_rank:
+        f0 = NF * d * 128
+
+        def load_piece(qn, k, which):
+            src, dst = (T.w1, T.wa) if which == 0 else (T.w2, T.wb)
+            q = queues[qn]
+            piece[k] = dma(q.dma_start(dst[:, 512 * k:512 * k + 512], src[:, f0 + 512 * k:f0 + 512 * k + 512]), "w%d" % k)
+
+        for i in range(8):
+            qn = ("sy", "s")[i % 2]
+            tk8 = dma(queues[qn].dma_start(T.k8[16 * i:16 * i + 16, :], T.keep[:, 16 * i:16 * i + 16]), "d_k8")
+        load_piece("sy", 0, 0)
+        load_piece("s", 0, 1)
+        tx = dma(g.sync.dma_start(T.xr[:, 4:RES], T.x[:, :]), "d_x")
+        tki = dma(g.sync.dma_start(T.ki[0:16, :], T.keep[:, :]), "d_ki")
+
+        idx, im, gm = [T.ii[:, i:i + 1] for i in range(3)]
+        e0, e8, g256, w8, wt, imf, base = [T.ff[:, i:i + 1] for i in range(7)]
+        jt, dj, sc, t1, t2, t3, t4 = [T.ts[:, 16 * i:16 * i + 16] for i in range(7)]
+        t_ones = done("v", V.memset(T.ones[:, :], 1.0))
+        t_idx = done("g", g.iota(idx, [[1, 1]], 0, 1))
+        need("g", t_ones)
+        t_mb = done("g", g.affine_select(T.mb[:, :], T.ones[:, :], [[16, 8], [0, 16]], ge, 0.0, -1, -1))
+        t_me = done("g", g.affine_select(T.me[:, :], T.ones[:, :], [[16, 8], [0, 16]], ge, 0.0, 15, -1))
+        t_mu = done("g", g.affine_select(T.mu[:, :], T.ones[:, :], [[1, 128]], ge, 0.0, 0, -1))
+        t_dj = done("g", g.iota(dj, [[-16, 16]], (-2049, 0)[d], -1, allow_small_or_imprecise_dtypes=True))
+        t_jt = done("g", g.iota(jt, [[16, 16]], 2048, 1, allow_small_or_imprecise_dtypes=True))
+        t_val0 = done("g", g.iota(T.val0[:, :], [[1, 256]], 1, 0, allow_small_or_imprecise_dtypes=True))
+        done("v", V.memset(T.onef[:, :], 1.0))
+        t_z = done("v", V.memset(T.xr[:, 0:4], 0.0))
+        done("v", V.memset(T.q[:, :], 0.0))
+        t_sl0 = done("v", V.memset(T.sl[:, :], 0.0))
+        need("v", t_idx)
+        done("v", V.tensor_scalar(im, idx, 15, None, AluOpType.bitwise_and))
+        t = done("v", V.tensor_scalar(gm, idx, 4, None, AluOpType.arith_shift_right))
+        need("v", t)
+        eq = AluOpType.is_equal
+        done("v", V.tensor_scalar(e0, im, 0, None, eq))
+        done("v", V.tensor_scalar(e8, im, 8, None, eq))
+        done("v", V.tensor_copy(imf, im))
+        t = done("v", V.tensor_scalar(g256, gm, 256, None, mult))
+        need("v", t)
+        t = done("v", V.tensor_tensor(w8, g256, e8, mult))
+        need("v", t)
+        t = done("v", V.tensor_tensor(wt, w8, e0, add))
+        need("v", t)
+        t_q = done("v", V.tensor_scalar(T.q[:, 0:144:16], T.onef[:, 0:9], wt, None, mult))
+
+        need("v", tk8)
+        t_kb = done("v", V.tensor_copy(T.k8b[:, :], T.k8[:, :]))
+        t_kn = done("v", V.tensor_scalar(T.k8n[:, :], T.k8[:, :], -1.0, None, mult))
+        kp, kn = (T.k8b, T.k8n) if d == 0 else (T.k8n, T.k8b)
+        need("pe", t_kb, t_kn, t_mb, t_me, t_mu)
+        PE.matmul(T.lb[:, 32:48], T.mb[:, :], kp[:, :], True, True)
+        PE.matmul(T.lb[:, 0:16], T.me[:, :], kp[:, :], True, False)
+        PE.matmul(T.lb[:, 0:16], T.mb[:, :], kn[:, :], False, True)
+        PE.matmul(T.lb[:, 16:32], T.mu[:, :], kp[:, :], True, False)
+        t_pre = done("pe", PE.matmul(T.lb[:, 16:32], T.me[:, :], kn[:, :], False, True))
+        need("v", t_val0)
+        t_val = done("v", V.tensor_scalar(T.val[:, :], T.val0[:, :], e0, e8, mult, add))
+        need("v", t_pre)
+        t = done("v", V.tensor_reduce(base, T.lb[:, 32:48], AxisListType.X, add))
+        need("v", t)
+        t = done("v", V.tensor_tensor_scan(sc, T.onef[:, 0:16], T.lb[:, 0:16], base, mult, add))
+        need("v", t, t_dj)
+        t = lb_free = done("v", V.tensor_tensor(t1, T.lb[:, 16:32], sc, add))
+        need("v", t)
+        t = done("v", V.tensor_tensor(t2, t1, dj, add))
+        need("v", t)
+        t = done("v", V.tensor_tensor(t3, t2, T.k8b[:, :], mult))
+        need("v", t, t_jt)
+        t = done("v", V.tensor_tensor(t4, t3, jt, add))
+        need("v", t)
+        t_off = done("v", V.tensor_copy(T.off[:, :], t4))
+        need("v", t_off, t_val, t_sl0)
+        t_sc = done("v", V.tensor_copy(T.sl[:, 0:SLW].indirect(T.off[:, 0:16]), T.val[:, :]))
+        need("pe", t_sc, t_q)
+        halves = [1 - d, d]
+        for h in halves:
+            for i in range(16):
+                m = PE.matmul(T["hb%d" % h][:, 0:64], T.q[:, 16 - i:144 - i], T.sl[:, 128 * i + 64 * h:128 * i + 64 * h + 64],
+                              i == 0, i == 15)
+            lists[h] = done("pe", m)
+        gath = {}
+        for h in halves:
+            need("v", lists[h])
+            lists[h] = hb_free[h] = done("v", V.tensor_copy(T.lo[:, 64 * h:64 * h + 64], T["hb%d" % h][:, 0:64]))
+            need("v", lists[h], tx, t_z)
+            tv = done("v", V.tensor_copy(T.pk[:, 1024 * h:1024 * h + 512], T.xr[:, 3:RES].indirect(T.lo[:, 64 * h:64 * h + 32])))
+            need("s", lists[h], tx, t_z)
+            ts = done("s", S.activation(T.pk[:, 1024 * h + 512:1024 * h + 1024],
+                                        T.xr[:, 3:RES].indirect(T.lo[:, 64 * h + 32:64 * h + 64]), Copy))
+            gath[h] = (tv, ts)
+
+        need("g", piece[0])
+        send_piece(0, [dies[d][relay[0]]])
+        for h in halves:
+            need("g", *gath[h])
+            send([([dies[h][j]], T.pk[:, 1024 * h + 256 * j:1024 * h + 256 * j + 256], T["tk%d" % d][:, :], "tk%d" % d)
+                  for j in range(4) if dies[h][j] != core], 4)
+        need("sy", *gath[halves[1]])
+        for k in range(1, PIECES):
+            load_piece("sy", k, 0)
+            load_piece("sy", k, 1)
+            if k + 1 < PIECES:
+                need("sy", piece[k])
+
+        t_r1 = done("g", g.affine_select(T.r1[0:16, :], T.ones[0:16, :], [[0, 8], [1, 16]], eq, 0.0, 0, -1))
+        t_ut = done("g", g.affine_select(T.ut[0:16, :], T.ones[0:16, :], [[0, 8], [1, 16]], ge, 0.0, 0, -1))
+        tt0, tt, rsc, rp, rc, rd, rf, rg, rh = [T.rr[:, 128 * i:128 * i + 128] for i in range(9)]
+        rs, ra, rb = [T.ri[:, 128 * i:128 * i + 128] for i in range(3)]
+        t_tt = done("g", g.iota(tt0, [[16, 128]], 0, 0, allow_small_or_imprecise_dtypes=True))
+        need("v", tki)
+        ta = done("v", V.tensor_copy(T.kib[0:16, :], T.ki[0:16, :]))
+        tb = done("v", V.tensor_scalar(T.kin[0:16, :], T.ki[0:16, :], -1.0, None, mult))
+        kp, kn = (T.kib, T.kin) if d == 0 else (T.kin, T.kib)
+        need("pe", ta, tb, t_r1, t_ut, lb_free)
+        PE.matmul(T.lb[:, 0:128], T.r1[0:16, :], T.kib[0:16, :], True, True)
+        PE.matmul(T.lb[:, 128:256], T.ones[0:16, :], kp[0:16, :], True, True)
+        PE.matmul(T.lb[:, 256:384], T.ut[0:16, :], kp[0:16, :], True, False)
+        t_pe = done("pe", PE.matmul(T.lb[:, 256:384], T.ones[0:16, :], kn[0:16, :], False, True))
+        need("v", t_tt)
+        t_t = done("v", V.tensor_scalar(tt, tt0, imf, None, add))
+        need("v", t_pe)
+        t = done("v", V.tensor_tensor_scan(rsc, T.onef[:, :], T.lb[:, 128:256], 0.0, mult, add))
+        need("v", t)
+        t = done("v", V.tensor_tensor(rp, T.lb[:, 256:384], rsc, add))
+        need("v", t)
+        t = done("v", V.tensor_scalar(rs, rp, (-1.0, 2048.0)[d], None, add))
+        need("v", t)
+        t = done("v", V.tensor_scalar(ra, rs, 127, None, AluOpType.bitwise_and))
+        tb = done("v", V.tensor_scalar(rb, rs, 7, None, AluOpType.arith_shift_right))
+        need("v", t)
+        t = done("v", V.tensor_scalar(rc, ra, 16.0, 2048.0, mult, add))
+        need("v", t, tb)
+        t = done("v", V.tensor_tensor(rd, rc, rb, add))
+        need("v", t, t_t)
+        t = done("v", V.tensor_tensor(rf, rd, tt, sub))
+        need("v", t)
+        t = done("v", V.tensor_tensor(rg, T.lb[:, 0:128], rf, mult))
+        need("v", t)
+        t = done("v", V.tensor_tensor(rh, rg, tt, add))
+        need("v", t)
+        t_ro = done("v", V.tensor_copy(T.ro[:, :], rh))
+    else:
+        for k in range(PIECES):
+            piece[k] = expect("w%d" % k, 16)
+        pass_on(0)
+
+    if is_rank:
+        need("v", expect("tk%d" % (1 - d), 4), *gath[d])
+        t_xm = done("v", V.tensor_tensor(T.xx[:, 0:256], T.pk[:, 1024 * d:1024 * d + 256], T["tk%d" % (1 - d)][:, :], add))
+    else:
+        need("v", expect("tk0", 4), expect("tk1", 4))
+        t_xm = done("v", V.tensor_tensor(T.xx[:, 0:256], T.tk0[:, :], T.tk1[:, :], add))
+    need("g", t_xm)
+    send([([partner], T.xx[:, 0:256], T.xx[:, 256:512], "xf")], 1)
+    xready = (t_xm, expect("xf", 16))
+    for k in range(1, PIECES):
+        if is_rank:
+            need("g", piece[k])
+            send_piece(k, [dies[d][relay[k]]])
+        else:
+            pass_on(k)
+
+    units = [(f, (0,)) for f in range(4)] + [(f, (1,)) for f in range(4)] + [(f, (0, 1)) for f in range(4, 12)] + \
+            [(f, (1,)) for f in range(12, 16)] + [(f, (0,)) for f in range(12, 16)]
+    U = len(units)
+    t_hr, t_l2 = [None] * U, [None] * U
+    first, last = {}, {}
+    for u, (f, subs) in enumerate(units):
+        for s in subs:
+            first.setdefault(s, u)
+            last[s] = u
+    for step in range(U + LOOK):
+        if step < U:
+            u = step
+            f, subs = units[u]
+            n, c0 = 256 * len(subs), 256 * subs[0]
+            hb, hr = T["hb%d" % (u % NH)], T["hr%d" % (u % NR)]
+            need("pe", hb_free[u % NH], piece[f // 4], *[xready[s] for s in subs])
+            t = done("pe", PE.matmul(hb[:, 0:n], T.wa[:, 128 * f:128 * f + 128], T.xx[:, c0:c0 + n], True, True))
+            need("s", t, t_l2[u - NR] if u >= NR else None)
+            t_hr[u] = hb_free[u % NH] = done("s", S.activation(hr[:, 0:n], hb[:, 0:n], Relu))
+        if step >= LOOK:
+            u = step - LOOK
+            f, subs = units[u]
+            hr = T["hr%d" % (u % NR)]
+            need("pe", t_hr[u])
+            for i, s in enumerate(subs):
+                m = PE.matmul(T["yb%d" % s][:, 0:256], T.wb[:, 128 * f:128 * f + 128], hr[:, 256 * i:256 * i + 256],
+                              u == first[s], u == last[s])
+            t_l2[u] = done("pe", m)
+            if u == last[1]:
+                need("v", t_l2[u])
+                t = done("v", V.tensor_copy(T.yo[:, :], T.yb1[:, 0:256]))
+                need("g", t)
+                send([([partner], T.yo[:, :], T.yp[:, :], "yp")], 1)
+    j0 = RES + 1024 * d + 256 * w
+    dst = T.xr[:, j0:j0 + 256]
+    src = dst if is_rank else T.ys[:, :]
+    need("v", t_l2[U - 1], expect("yp", 16))
+    t_y = done("v", V.tensor_tensor(src, T.yb0[:, 0:256], T.yp[:, :], add))
+    need("g", t_y)
+    send([([r for r in ranks if r != core], src, dst, "res")], 1)
+
+    if is_rank:
+        t_res = expect("res", 7 * 16)
+        need("v", t_res, t_ro, t_y)
+        tv = done("v", V.tensor_copy(T.yt[:, 0:1024], T.xr[:, 4:4100].indirect(T.ro[:, 0:64])))
+        need("s", t_res, t_ro, t_y)
+        ts = done("s", S.activation(T.yt[:, 1024:2048], T.xr[:, 4:4100].indirect(T.ro[:, 64:128]), Copy))
+        need("sy", tv)
+        dma(g.sync.dma_start(T.y[:, 0:1024], T.yt[:, 0:1024]), "d_st")
+        need("s", ts)
+        dma(g.scalar.dma_start(T.y[:, 1024:2048], T.yt[:, 1024:2048]), "d_st")
+    for s in sorted(total):
+        if seen.get(s, 0) < total[s]:
+            need("g", (s, total[s]))

@@ -5,15 +5,16 @@ NF = 16
 PIECES = 4
 NH = 5
 NR = 5
-LOOK = 2
+LOOK = 3
 SLW = 2048 + 368
 RES = 2052
 
 SCRATCH = {
-    "k8": ("sbuf", [128, 16], "int32"), "k8b": ("sbuf", [128, 16], "bfloat16"), "k8n": ("sbuf", [128, 16], "bfloat16"),
+    "k8": ("sbuf", [128, 16], "int32"), "k8o": ("sbuf", [128, 16], "int32"), "k8s": ("sbuf", [128, 16], "bfloat16"),
+    "k8b": ("sbuf", [128, 16], "bfloat16"), "k8n": ("sbuf", [128, 16], "bfloat16"),
     "ki": ("sbuf", [128, 128], "int32"), "kib": ("sbuf", [128, 128], "bfloat16"), "kin": ("sbuf", [128, 128], "bfloat16"),
-    "ones": ("sbuf", [128, 128], "bfloat16"), "onef": ("sbuf", [128, 128], "float32"),
-    "mu": ("sbuf", [128, 128], "bfloat16"), "me": ("sbuf", [128, 128], "bfloat16"), "mb": ("sbuf", [128, 128], "bfloat16"),
+    "ones": ("sbuf", [128, 144], "bfloat16"), "onef": ("sbuf", [128, 128], "float32"),
+    "mu": ("sbuf", [128, 128], "bfloat16"), "mb": ("sbuf", [128, 144], "bfloat16"),
     "r1": ("sbuf", [128, 128], "bfloat16"), "ut": ("sbuf", [128, 128], "bfloat16"),
     "ii": ("sbuf", [128, 4], "int32"),
     "ff": ("sbuf", [128, 8], "float32"),
@@ -25,15 +26,16 @@ SCRATCH = {
     "xr": ("sbuf", [128, 4100], "float32"), "pk": ("sbuf", [128, 2048], "float32"), "yt": ("sbuf", [128, 2048], "float32"),
     "wa": ("sbuf", [128, 2048], "float32"), "wb": ("sbuf", [128, 2048], "float32"),
     "tk0": ("sbuf", [128, 256], "float32"), "tk1": ("sbuf", [128, 256], "float32"),
-    "xx": ("sbuf", [128, 512], "float32"),
-    "yo": ("sbuf", [128, 256], "float32"), "yp": ("sbuf", [128, 256], "float32"), "ys": ("sbuf", [128, 256], "float32"),
+    "xa": ("sbuf", [128, 128], "float32"), "xb": ("sbuf", [128, 128], "float32"), "xc": ("sbuf", [128, 128], "float32"),
+    "xx": ("sbuf", [128, 256], "float32"),
+    "yo": ("sbuf", [128, 128], "float32"), "yp": ("sbuf", [128, 128], "float32"), "ys": ("sbuf", [128, 128], "float32"),
     "yb0": ("psum", [128, 512], "float32"), "yb1": ("psum", [128, 512], "float32"), "lb": ("psum", [128, 512], "float32"),
 }
 for _i in range(NH):
     SCRATCH["hb%d" % _i] = ("psum", [128, 512], "float32")
 for _i in range(NR):
-    SCRATCH["hr%d" % _i] = ("sbuf", [128, 512], "float32")
-SEMAPHORES = ["c_pe", "c_v", "c_s", "c_g", "d_k8", "d_x", "d_ki", "d_st", "snd", "tk0", "tk1", "xf", "yp", "res"] + \
+    SCRATCH["hr%d" % _i] = ("sbuf", [128, 256], "float32")
+SEMAPHORES = ["c_pe", "c_v", "c_s", "c_g", "d_k8", "d_x", "d_ki", "d_st", "snd", "tk0", "tk1", "ko", "xc", "xf", "yp", "res"] + \
     ["w%d" % k for k in range(PIECES)]
 
 
@@ -41,17 +43,28 @@ def rank_program(g, core, T, topo):
     def place(c):
         return (topo.host(c), topo.chip(c))
 
-    ranks = [c for c in T.cores if place(c) == place(core)]
-    if not ranks:
+    chips = []
+    for c in T.cores:
+        if all(place(c) != place(rs[0]) for rs in chips):
+            chips.append([r for r in T.cores if place(r) == place(c)])
+    here = [i for i in range(len(chips)) if place(chips[i][0]) == place(core)]
+    if not here:
         return
-    mine = [c for c in range(256) if place(c) == place(core)]
-    dies = [[r] + [c for c in mine if topo.die(c) == topo.die(r) and c != r] for r in ranks]
+    q = here[0]
+
+    def dies_of(rs):
+        mine = [c for c in range(256) if place(c) == place(rs[0])]
+        return [[r] + [c for c in mine if topo.die(c) == topo.die(r) and c != r] for r in rs]
+
+    ranks, dies = chips[q], dies_of(chips[q])
     d = [i for i in range(2) if core in dies[i]][0]
     w = dies[d].index(core)
     is_rank = w == 0
     partner = dies[1 - d][w]
+    across = dies_of(chips[1 - q])[d][w]
 
     add, sub, mult = AluOpType.add, AluOpType.subtract, AluOpType.mult
+    ge, eq = AluOpType.is_ge, AluOpType.is_equal
     Copy, Relu = ActivationFunctionType.Copy, ActivationFunctionType.Relu
     V, S, PE = g.vector, g.scalar, g.tensor
     queues = {"pe": g.tensor, "v": g.vector, "s": g.scalar, "g": g, "sy": g.sync}
@@ -80,13 +93,11 @@ def rank_program(g, core, T, topo):
         inst.then_inc(T.sem[s], 16)
         return expect(s, 16)
 
-    def parts(n, dsts):
+    def engines(dsts):
         m = topo.mask(core, dsts[0])
         for c in dsts:
             m &= topo.mask(core, c)
-        bits = [1 << i for i in range(16) if (m >> i) & 1]
-        k = len(bits) // n
-        return [sum(bits[i * k:(i + 1) * k]) for i in range(n)], k
+        return [1 << i for i in range(16) if (m >> i) & 1]
 
     def ids(dsts):
         out = []
@@ -95,14 +106,21 @@ def rank_program(g, core, T, topo):
             out.append(DstId(rid=rid, pnc=pid))
         return out
 
-    def send(items, n):
+    def fused(items):
         tr = []
-        for j, (dsts, src, dst, s) in enumerate(items):
-            ms, k = parts(n, dsts)
+        for dsts, src, dst, s, bits in items:
             tr.append(RemoteDMATransfer(dst_ids=ids(dsts), srcs=[src], dsts=[dst for _ in dsts],
-                                        dma_engine_mask=ms[j], remote_sem=T.sem[s]))
-            expect("snd", k)
+                                        dma_engine_mask=sum(bits), remote_sem=T.sem[s]))
+            expect("snd", len(bits))
         g.remote_dma_fused(tr, local_sem=T.sem["snd"])
+
+    def send(items, n):
+        full = []
+        for j, it in enumerate(items):
+            e = engines(it[0])
+            k = len(e) // n
+            full.append(it + (e[j * k:(j + 1) * k],))
+        fused(full)
 
     def send_piece(k, dsts):
         c = slice(512 * k, 512 * k + 512)
@@ -112,20 +130,22 @@ def rank_program(g, core, T, topo):
     piece = [None] * PIECES
 
     def pass_on(k):
-        if not is_rank and w == relay[k]:
+        if is_rank:
+            need("g", piece[k])
+            send_piece(k, [dies[d][relay[k]]])
+        elif w == relay[k]:
             need("g", piece[k])
             send_piece(k, [dies[d][j] for j in (1, 2, 3) if j != w])
 
     lists = {}
     hb_free = [None] * NH
-    ge = AluOpType.is_ge
     if is_rank:
         f0 = NF * d * 128
 
         def load_piece(qn, k, which):
             src, dst = (T.w1, T.wa) if which == 0 else (T.w2, T.wb)
-            q = queues[qn]
-            piece[k] = dma(q.dma_start(dst[:, 512 * k:512 * k + 512], src[:, f0 + 512 * k:f0 + 512 * k + 512]), "w%d" % k)
+            piece[k] = dma(queues[qn].dma_start(dst[:, 512 * k:512 * k + 512], src[:, f0 + 512 * k:f0 + 512 * k + 512]),
+                           "w%d" % k)
 
         for i in range(8):
             qn = ("sy", "s")[i % 2]
@@ -136,16 +156,18 @@ def rank_program(g, core, T, topo):
         tki = dma(g.sync.dma_start(T.ki[0:16, :], T.keep[:, :]), "d_ki")
 
         idx, im, gm = [T.ii[:, i:i + 1] for i in range(3)]
-        e0, e8, g256, w8, wt, imf, base = [T.ff[:, i:i + 1] for i in range(7)]
+        e0, e8, g256, w8, wt, imf, base, cnt = [T.ff[:, i:i + 1] for i in range(8)]
         jt, dj, sc, t1, t2, t3, t4 = [T.ts[:, 16 * i:16 * i + 16] for i in range(7)]
         t_ones = done("v", V.memset(T.ones[:, :], 1.0))
         t_idx = done("g", g.iota(idx, [[1, 1]], 0, 1))
         need("g", t_ones)
-        t_mb = done("g", g.affine_select(T.mb[:, :], T.ones[:, :], [[16, 8], [0, 16]], ge, 0.0, -1, -1))
-        t_me = done("g", g.affine_select(T.me[:, :], T.ones[:, :], [[16, 8], [0, 16]], ge, 0.0, 15, -1))
-        t_mu = done("g", g.affine_select(T.mu[:, :], T.ones[:, :], [[1, 128]], ge, 0.0, 0, -1))
-        t_dj = done("g", g.iota(dj, [[-16, 16]], (-2049, 0)[d], -1, allow_small_or_imprecise_dtypes=True))
+        t_mb = done("g", g.affine_select(T.mb[:, :], T.ones[:, :], [[16, 9], [0, 16]], ge, 0.0, -1, -1))
+        t_mu = done("g", g.affine_select(T.mu[:, :], T.ones[:, 0:128], [[1, 128]], ge, 0.0, 0, -1))
         t_jt = done("g", g.iota(jt, [[16, 16]], 2048, 1, allow_small_or_imprecise_dtypes=True))
+        mb, me = T.mb[:, 0:128], T.mb[:, 16:144]
+        if d == 0:
+            need("g", tk8)
+            send([([partner], T.k8[:, :], T.k8o[:, :], "ko")], 1)
         t_val0 = done("g", g.iota(T.val0[:, :], [[1, 256]], 1, 0, allow_small_or_imprecise_dtypes=True))
         done("v", V.memset(T.onef[:, :], 1.0))
         t_z = done("v", V.memset(T.xr[:, 0:4], 0.0))
@@ -155,7 +177,6 @@ def rank_program(g, core, T, topo):
         done("v", V.tensor_scalar(im, idx, 15, None, AluOpType.bitwise_and))
         t = done("v", V.tensor_scalar(gm, idx, 4, None, AluOpType.arith_shift_right))
         need("v", t)
-        eq = AluOpType.is_equal
         done("v", V.tensor_scalar(e0, im, 0, None, eq))
         done("v", V.tensor_scalar(e8, im, 8, None, eq))
         done("v", V.tensor_copy(imf, im))
@@ -164,21 +185,26 @@ def rank_program(g, core, T, topo):
         t = done("v", V.tensor_tensor(w8, g256, e8, mult))
         need("v", t)
         t = done("v", V.tensor_tensor(wt, w8, e0, add))
-        need("v", t)
+        need("v", t, t_jt)
+        t_dj = done("v", V.tensor_scalar(dj, jt, -1.0, (-1.0, 2048.0)[q], mult, add))
         t_q = done("v", V.tensor_scalar(T.q[:, 0:144:16], T.onef[:, 0:9], wt, None, mult))
 
         need("v", tk8)
         t_kb = done("v", V.tensor_copy(T.k8b[:, :], T.k8[:, :]))
         t_kn = done("v", V.tensor_scalar(T.k8n[:, :], T.k8[:, :], -1.0, None, mult))
-        kp, kn = (T.k8b, T.k8n) if d == 0 else (T.k8n, T.k8b)
-        need("pe", t_kb, t_kn, t_mb, t_me, t_mu)
-        PE.matmul(T.lb[:, 32:48], T.mb[:, :], kp[:, :], True, True)
-        PE.matmul(T.lb[:, 0:16], T.me[:, :], kp[:, :], True, False)
-        PE.matmul(T.lb[:, 0:16], T.mb[:, :], kn[:, :], False, True)
+        kp, kn = (T.k8b, T.k8n) if q == 0 else (T.k8n, T.k8b)
+        need("pe", t_kb, t_kn, t_mb, t_mu)
+        PE.matmul(T.lb[:, 0:16], me, kp[:, :], True, False)
+        PE.matmul(T.lb[:, 0:16], mb, kn[:, :], False, True)
         PE.matmul(T.lb[:, 16:32], T.mu[:, :], kp[:, :], True, False)
-        t_pre = done("pe", PE.matmul(T.lb[:, 16:32], T.me[:, :], kn[:, :], False, True))
-        need("v", t_val0)
-        t_val = done("v", V.tensor_scalar(T.val[:, :], T.val0[:, :], e0, e8, mult, add))
+        PE.matmul(T.lb[:, 16:32], me, kn[:, :], False, True)
+        m = PE.matmul(T.lb[:, 32:48], mb, kp[:, :], True, d == 0)
+        if d == 1:
+            need("v", expect("ko", 16))
+            t_ks = done("v", V.tensor_scalar(T.k8s[:, :], T.k8o[:, :], (1.0, -1.0)[q], None, mult))
+            need("pe", t_ks)
+            m = PE.matmul(T.lb[:, 32:48], T.ones[:, 0:128], T.k8s[:, :], False, True)
+        t_pre = done("pe", m)
         need("v", t_pre)
         t = done("v", V.tensor_reduce(base, T.lb[:, 32:48], AxisListType.X, add))
         need("v", t)
@@ -193,6 +219,8 @@ def rank_program(g, core, T, topo):
         t = done("v", V.tensor_tensor(t4, t3, jt, add))
         need("v", t)
         t_off = done("v", V.tensor_copy(T.off[:, :], t4))
+        need("v", t_val0)
+        t_val = done("v", V.tensor_scalar(T.val[:, :], T.val0[:, :], e0, e8, mult, add))
         need("v", t_off, t_val, t_sl0)
         t_sc = done("v", V.tensor_copy(T.sl[:, 0:SLW].indirect(T.off[:, 0:16]), T.val[:, :]))
         need("pe", t_sc, t_q)
@@ -213,8 +241,7 @@ def rank_program(g, core, T, topo):
                                         T.xr[:, 3:RES].indirect(T.lo[:, 64 * h + 32:64 * h + 64]), Copy))
             gath[h] = (tv, ts)
 
-        need("g", piece[0])
-        send_piece(0, [dies[d][relay[0]]])
+        pass_on(0)
         for h in halves:
             need("g", *gath[h])
             send([([dies[h][j]], T.pk[:, 1024 * h + 256 * j:1024 * h + 256 * j + 256], T["tk%d" % d][:, :], "tk%d" % d)
@@ -226,28 +253,34 @@ def rank_program(g, core, T, topo):
             if k + 1 < PIECES:
                 need("sy", piece[k])
 
-        t_r1 = done("g", g.affine_select(T.r1[0:16, :], T.ones[0:16, :], [[0, 8], [1, 16]], eq, 0.0, 0, -1))
-        t_ut = done("g", g.affine_select(T.ut[0:16, :], T.ones[0:16, :], [[0, 8], [1, 16]], ge, 0.0, 0, -1))
+        t_r1 = done("g", g.affine_select(T.r1[0:16, :], T.ones[0:16, 0:128], [[0, 8], [1, 16]], eq, 0.0, 0, -1))
+        t_ut = done("g", g.affine_select(T.ut[0:16, :], T.ones[0:16, 0:128], [[0, 8], [1, 16]], ge, 0.0, 0, -1))
         tt0, tt, rsc, rp, rc, rd, rf, rg, rh = [T.rr[:, 128 * i:128 * i + 128] for i in range(9)]
         rs, ra, rb = [T.ri[:, 128 * i:128 * i + 128] for i in range(3)]
         t_tt = done("g", g.iota(tt0, [[16, 128]], 0, 0, allow_small_or_imprecise_dtypes=True))
         need("v", tki)
         ta = done("v", V.tensor_copy(T.kib[0:16, :], T.ki[0:16, :]))
         tb = done("v", V.tensor_scalar(T.kin[0:16, :], T.ki[0:16, :], -1.0, None, mult))
-        kp, kn = (T.kib, T.kin) if d == 0 else (T.kin, T.kib)
+        kp, kn = (T.kib, T.kin) if q == 0 else (T.kin, T.kib)
         need("pe", ta, tb, t_r1, t_ut, lb_free)
         PE.matmul(T.lb[:, 0:128], T.r1[0:16, :], T.kib[0:16, :], True, True)
-        PE.matmul(T.lb[:, 128:256], T.ones[0:16, :], kp[0:16, :], True, True)
+        if d == 1:
+            PE.matmul(T.lb[:, 384:400], T.ones[:, 0:128], T.k8s[:, :], True, True)
+        PE.matmul(T.lb[:, 128:256], T.ones[0:16, 0:128], kp[0:16, :], True, True)
         PE.matmul(T.lb[:, 256:384], T.ut[0:16, :], kp[0:16, :], True, False)
-        t_pe = done("pe", PE.matmul(T.lb[:, 256:384], T.ones[0:16, :], kn[0:16, :], False, True))
+        t_pe = done("pe", PE.matmul(T.lb[:, 256:384], T.ones[0:16, 0:128], kn[0:16, :], False, True))
         need("v", t_tt)
         t_t = done("v", V.tensor_scalar(tt, tt0, imf, None, add))
         need("v", t_pe)
-        t = done("v", V.tensor_tensor_scan(rsc, T.onef[:, :], T.lb[:, 128:256], 0.0, mult, add))
+        start = 0.0
+        if d == 1:
+            start = cnt
+            need("v", done("v", V.tensor_reduce(cnt, T.lb[:, 384:400], AxisListType.X, add)))
+        t = done("v", V.tensor_tensor_scan(rsc, T.onef[:, :], T.lb[:, 128:256], start, mult, add))
         need("v", t)
         t = done("v", V.tensor_tensor(rp, T.lb[:, 256:384], rsc, add))
         need("v", t)
-        t = done("v", V.tensor_scalar(rs, rp, (-1.0, 2048.0)[d], None, add))
+        t = done("v", V.tensor_scalar(rs, rp, (-1.0, 2048.0)[q], None, add))
         need("v", t)
         t = done("v", V.tensor_scalar(ra, rs, 127, None, AluOpType.bitwise_and))
         tb = done("v", V.tensor_scalar(rb, rs, 7, None, AluOpType.arith_shift_right))
@@ -268,24 +301,29 @@ def rank_program(g, core, T, topo):
             piece[k] = expect("w%d" % k, 16)
         pass_on(0)
 
-    if is_rank:
-        need("v", expect("tk%d" % (1 - d), 4), *gath[d])
-        t_xm = done("v", V.tensor_tensor(T.xx[:, 0:256], T.pk[:, 1024 * d:1024 * d + 256], T["tk%d" % (1 - d)][:, :], add))
-    else:
-        need("v", expect("tk0", 4), expect("tk1", 4))
-        t_xm = done("v", V.tensor_tensor(T.xx[:, 0:256], T.tk0[:, :], T.tk1[:, :], add))
-    need("g", t_xm)
-    send([([partner], T.xx[:, 0:256], T.xx[:, 256:512], "xf")], 1)
-    xready = (t_xm, expect("xf", 16))
-    for k in range(1, PIECES):
-        if is_rank:
-            need("g", piece[k])
-            send_piece(k, [dies[d][relay[k]]])
-        else:
-            pass_on(k)
+    ca, cb = slice(128 * (1 - q), 128 * (1 - q) + 128), slice(128 * q, 128 * q + 128)
 
-    units = [(f, (0,)) for f in range(4)] + [(f, (1,)) for f in range(4)] + [(f, (0, 1)) for f in range(4, 12)] + \
-            [(f, (1,)) for f in range(12, 16)] + [(f, (0,)) for f in range(12, 16)]
+    def part(r, c):
+        return T.pk[:, 1024 * d + c.start:1024 * d + c.stop] if is_rank and r == d else T["tk%d" % r][:, c]
+
+    deps = list(gath[d]) if is_rank else [expect("tk%d" % d, 4)]
+    need("v", expect("tk%d" % (1 - d), 4), *deps)
+    t_xa = done("v", V.tensor_tensor(T.xa[:, :], part(0, ca), part(1, ca), add))
+    t_xb = done("v", V.tensor_tensor(T.xb[:, :], part(0, cb), part(1, cb), add))
+    need("g", t_xa)
+    send([([across], T.xa[:, :], T.xc[:, :], "xc")], 1)
+    if is_rank:
+        pass_on(1)
+    need("v", t_xb, expect("xc", len(engines([across]))))
+    t_xm = done("v", V.tensor_tensor(T.xx[:, 0:128], T.xb[:, :], T.xc[:, :], add))
+    need("g", t_xm)
+    send([([partner], T.xx[:, 0:128], T.xx[:, 128:256], "xf")], 1)
+    xready = (t_xm, expect("xf", 16))
+    for k in range(2 if is_rank else 1, PIECES):
+        pass_on(k)
+
+    units = [(f, (0,)) for f in range(4)] + [(f, (1,)) for f in range(4)] + [(f, (0, 1)) for f in range(4, 10)] + \
+            [(f, (1,)) for f in range(10, 16)] + [(f, (0,)) for f in range(10, 16)]
     U = len(units)
     t_hr, t_l2 = [None] * U, [None] * U
     first, last = {}, {}
@@ -297,7 +335,7 @@ def rank_program(g, core, T, topo):
         if step < U:
             u = step
             f, subs = units[u]
-            n, c0 = 256 * len(subs), 256 * subs[0]
+            n, c0 = 128 * len(subs), 128 * subs[0]
             hb, hr = T["hb%d" % (u % NH)], T["hr%d" % (u % NR)]
             need("pe", hb_free[u % NH], piece[f // 4], *[xready[s] for s in subs])
             t = done("pe", PE.matmul(hb[:, 0:n], T.wa[:, 128 * f:128 * f + 128], T.xx[:, c0:c0 + n], True, True))
@@ -309,24 +347,26 @@ def rank_program(g, core, T, topo):
             hr = T["hr%d" % (u % NR)]
             need("pe", t_hr[u])
             for i, s in enumerate(subs):
-                m = PE.matmul(T["yb%d" % s][:, 0:256], T.wb[:, 128 * f:128 * f + 128], hr[:, 256 * i:256 * i + 256],
+                m = PE.matmul(T["yb%d" % s][:, 0:128], T.wb[:, 128 * f:128 * f + 128], hr[:, 128 * i:128 * i + 128],
                               u == first[s], u == last[s])
             t_l2[u] = done("pe", m)
             if u == last[1]:
                 need("v", t_l2[u])
-                t = done("v", V.tensor_copy(T.yo[:, :], T.yb1[:, 0:256]))
+                t = done("v", V.tensor_copy(T.yo[:, :], T.yb1[:, 0:128]))
                 need("g", t)
                 send([([partner], T.yo[:, :], T.yp[:, :], "yp")], 1)
-    j0 = RES + 1024 * d + 256 * w
-    dst = T.xr[:, j0:j0 + 256]
+    j0 = RES + 1024 * d + 256 * w + 128 * q
+    dst = T.xr[:, j0:j0 + 128]
     src = dst if is_rank else T.ys[:, :]
     need("v", t_l2[U - 1], expect("yp", 16))
-    t_y = done("v", V.tensor_tensor(src, T.yb0[:, 0:256], T.yp[:, :], add))
+    t_y = done("v", V.tensor_tensor(src, T.yb0[:, 0:128], T.yp[:, :], add))
     need("g", t_y)
-    send([([r for r in ranks if r != core], src, dst, "res")], 1)
+    near, far = [r for r in ranks if r != core], chips[1 - q]
+    e_far = engines(far)
+    fused([(far, src, dst, "res", e_far), (near, src, dst, "res", [e for e in engines(near) if e not in e_far])])
 
     if is_rank:
-        t_res = expect("res", 7 * 16)
+        t_res = expect("res", 15 * 8)
         need("v", t_res, t_ro, t_y)
         tv = done("v", V.tensor_copy(T.yt[:, 0:1024], T.xr[:, 4:4100].indirect(T.ro[:, 0:64])))
         need("s", t_res, t_ro, t_y)

@@ -2,10 +2,12 @@ from concourse.bass import DstId, RemoteDMATransfer
 from concourse.mybir import AluOpType, AxisListType, ActivationFunctionType
 
 NF = 16
-PIECES = 4
+CUTS = (0, 2, 4, 6, 10, 13, 16)
+PIECES = 6
+EARLY = 3
 NH = 5
-NR = 5
-LOOK = 3
+NR = 6
+LOOK = 4
 SLW = 2048 + 368
 RES = 2052
 
@@ -19,24 +21,24 @@ SCRATCH = {
     "ii": ("sbuf", [128, 4], "int32"),
     "ff": ("sbuf", [128, 8], "float32"),
     "q": ("sbuf", [128, 144], "bfloat16"), "val0": ("sbuf", [128, 256], "bfloat16"), "val": ("sbuf", [128, 256], "bfloat16"),
-    "ts": ("sbuf", [128, 112], "float32"),
+    "ts": ("sbuf", [128, 128], "float32"),
     "off": ("sbuf", [128, 16], "uint16"),
     "sl": ("sbuf", [128, SLW], "bfloat16"), "lo": ("sbuf", [128, 128], "uint16"), "ro": ("sbuf", [128, 128], "uint16"),
-    "rr": ("sbuf", [128, 1152], "float32"), "ri": ("sbuf", [128, 384], "int32"),
+    "rr": ("sbuf", [128, 1280], "float32"), "ri": ("sbuf", [128, 384], "int32"),
     "xr": ("sbuf", [128, 4100], "float32"), "pk": ("sbuf", [128, 2048], "float32"), "yt": ("sbuf", [128, 2048], "float32"),
     "wa": ("sbuf", [128, 2048], "float32"), "wb": ("sbuf", [128, 2048], "float32"),
     "tk0": ("sbuf", [128, 256], "float32"), "tk1": ("sbuf", [128, 256], "float32"),
     "xa": ("sbuf", [128, 128], "float32"), "xb": ("sbuf", [128, 128], "float32"), "xc": ("sbuf", [128, 128], "float32"),
     "xx": ("sbuf", [128, 256], "float32"),
     "yo": ("sbuf", [128, 128], "float32"), "yp": ("sbuf", [128, 128], "float32"), "ys": ("sbuf", [128, 128], "float32"),
-    "yb0": ("psum", [128, 512], "float32"), "yb1": ("psum", [128, 512], "float32"), "lb": ("psum", [128, 512], "float32"),
+    "yb0": ("psum", [128, 512], "float32"), "yb1": ("psum", [128, 512], "float32"), "yb2": ("psum", [128, 512], "float32"),
 }
 for _i in range(NH):
     SCRATCH["hb%d" % _i] = ("psum", [128, 512], "float32")
 for _i in range(NR):
     SCRATCH["hr%d" % _i] = ("sbuf", [128, 256], "float32")
 SEMAPHORES = ["c_pe", "c_v", "c_s", "c_g", "d_k8", "d_x", "d_ki", "d_st", "snd", "tk0", "tk1", "ko", "xc", "xf", "yp", "res"] + \
-    ["w%d" % k for k in range(PIECES)]
+    ["w%d" % k for k in range(PIECES)] + ["v%d" % k for k in range(EARLY)]
 
 
 def rank_program(g, core, T, topo):
@@ -122,42 +124,55 @@ def rank_program(g, core, T, topo):
             full.append(it + (e[j * k:(j + 1) * k],))
         fused(full)
 
-    def send_piece(k, dsts):
-        c = slice(512 * k, 512 * k + 512)
-        send([(dsts, T.wa[:, c], T.wa[:, c], "w%d" % k), (dsts, T.wb[:, c], T.wb[:, c], "w%d" % k)], 2)
-
     relay = [1 + k % 3 for k in range(PIECES)]
-    piece = [None] * PIECES
+    piece = [[None, None] for _ in range(PIECES)]
+
+    def cols(k):
+        return slice(128 * CUTS[k], 128 * CUTS[k + 1])
+
+    def others(k):
+        return [dies[d][j] for j in (1, 2, 3) if j != relay[k]]
+
+    def early(which):
+        wt, nm = ((T.wa, "w%d"), (T.wb, "v%d"))[which]
+        if is_rank:
+            need("g", piece[0][which])
+            send([([dies[d][relay[k]]], wt[:, cols(k)], wt[:, cols(k)], nm % k) for k in range(EARLY)], 4)
+        else:
+            k = relay.index(w)
+            need("g", piece[k][which])
+            send([(others(k), wt[:, cols(k)], wt[:, cols(k)], nm % k)], 1)
 
     def pass_on(k):
-        if is_rank:
-            need("g", piece[k])
-            send_piece(k, [dies[d][relay[k]]])
-        elif w == relay[k]:
-            need("g", piece[k])
-            send_piece(k, [dies[d][j] for j in (1, 2, 3) if j != w])
+        if is_rank or w == relay[k]:
+            dsts = [dies[d][relay[k]]] if is_rank else others(k)
+            need("g", *piece[k])
+            send([(dsts, T.wa[:, cols(k)], T.wa[:, cols(k)], "w%d" % k), (dsts, T.wb[:, cols(k)], T.wb[:, cols(k)], "w%d" % k)], 2)
 
     lists = {}
     hb_free = [None] * NH
+    lb = T["hb%d" % (NH - 1)]
     if is_rank:
         f0 = NF * d * 128
 
-        def load_piece(qn, k, which):
+        def load(qn, k0, k1, which, s):
             src, dst = (T.w1, T.wa) if which == 0 else (T.w2, T.wb)
-            piece[k] = dma(queues[qn].dma_start(dst[:, 512 * k:512 * k + 512], src[:, f0 + 512 * k:f0 + 512 * k + 512]),
-                           "w%d" % k)
+            a, b = 128 * CUTS[k0], 128 * CUTS[k1]
+            tok = dma(queues[qn].dma_start(dst[:, a:b], src[:, f0 + a:f0 + b]), s)
+            for k in range(k0, k1):
+                piece[k][which] = tok
 
         for i in range(8):
             qn = ("sy", "s")[i % 2]
             tk8 = dma(queues[qn].dma_start(T.k8[16 * i:16 * i + 16, :], T.keep[:, 16 * i:16 * i + 16]), "d_k8")
-        load_piece("sy", 0, 0)
-        load_piece("s", 0, 1)
+        load("s", 0, EARLY, 0, "w0")
         tx = dma(g.sync.dma_start(T.xr[:, 4:RES], T.x[:, :]), "d_x")
         tki = dma(g.sync.dma_start(T.ki[0:16, :], T.keep[:, :]), "d_ki")
+        load("sy", 0, EARLY, 1, "v0")
 
         idx, im, gm = [T.ii[:, i:i + 1] for i in range(3)]
         e0, e8, g256, w8, wt, imf, base, cnt = [T.ff[:, i:i + 1] for i in range(8)]
-        jt, dj, sc, t1, t2, t3, t4 = [T.ts[:, 16 * i:16 * i + 16] for i in range(7)]
+        jt, dj, sc, t1, t2, t2b, t3, t4 = [T.ts[:, 16 * i:16 * i + 16] for i in range(8)]
         t_ones = done("v", V.memset(T.ones[:, :], 1.0))
         t_idx = done("g", g.iota(idx, [[1, 1]], 0, 1))
         need("g", t_ones)
@@ -167,7 +182,7 @@ def rank_program(g, core, T, topo):
         mb, me = T.mb[:, 0:128], T.mb[:, 16:144]
         if d == 0:
             need("g", tk8)
-            send([([partner], T.k8[:, :], T.k8o[:, :], "ko")], 1)
+            fused([([partner], T.k8[:, :], T.k8o[:, :], "ko", engines([partner])[0:8])])
         t_val0 = done("g", g.iota(T.val0[:, :], [[1, 256]], 1, 0, allow_small_or_imprecise_dtypes=True))
         done("v", V.memset(T.onef[:, :], 1.0))
         t_z = done("v", V.memset(T.xr[:, 0:4], 0.0))
@@ -194,33 +209,38 @@ def rank_program(g, core, T, topo):
         t_kn = done("v", V.tensor_scalar(T.k8n[:, :], T.k8[:, :], -1.0, None, mult))
         kp, kn = (T.k8b, T.k8n) if q == 0 else (T.k8n, T.k8b)
         need("pe", t_kb, t_kn, t_mb, t_mu)
-        PE.matmul(T.lb[:, 0:16], me, kp[:, :], True, False)
-        PE.matmul(T.lb[:, 0:16], mb, kn[:, :], False, True)
-        PE.matmul(T.lb[:, 16:32], T.mu[:, :], kp[:, :], True, False)
-        PE.matmul(T.lb[:, 16:32], me, kn[:, :], False, True)
-        m = PE.matmul(T.lb[:, 32:48], mb, kp[:, :], True, d == 0)
-        if d == 1:
-            need("v", expect("ko", 16))
-            t_ks = done("v", V.tensor_scalar(T.k8s[:, :], T.k8o[:, :], (1.0, -1.0)[q], None, mult))
-            need("pe", t_ks)
-            m = PE.matmul(T.lb[:, 32:48], T.ones[:, 0:128], T.k8s[:, :], False, True)
-        t_pre = done("pe", m)
+        PE.matmul(lb[:, 0:16], me, kp[:, :], True, False)
+        PE.matmul(lb[:, 0:16], mb, kn[:, :], False, True)
+        PE.matmul(lb[:, 16:32], T.mu[:, :], kp[:, :], True, False)
+        PE.matmul(lb[:, 16:32], me, kn[:, :], False, True)
+        t_pre = done("pe", PE.matmul(lb[:, 32:48], mb, kp[:, :], True, True))
         need("v", t_pre)
-        t = done("v", V.tensor_reduce(base, T.lb[:, 32:48], AxisListType.X, add))
+        t = done("v", V.tensor_reduce(base, lb[:, 32:48], AxisListType.X, add))
         need("v", t)
-        t = done("v", V.tensor_tensor_scan(sc, T.onef[:, 0:16], T.lb[:, 0:16], base, mult, add))
+        t = done("v", V.tensor_tensor_scan(sc, T.onef[:, 0:16], lb[:, 0:16], base, mult, add))
         need("v", t, t_dj)
-        t = lb_free = done("v", V.tensor_tensor(t1, T.lb[:, 16:32], sc, add))
+        t = lb_free = done("v", V.tensor_tensor(t1, lb[:, 16:32], sc, add))
         need("v", t)
         t = done("v", V.tensor_tensor(t2, t1, dj, add))
+        need("v", t_val0)
+        t_val = done("v", V.tensor_scalar(T.val[:, :], T.val0[:, :], e0, e8, mult, add))
+        ts2 = t2
+        if d == 1:
+            need("v", expect("ko", 8))
+            t_ks = done("v", V.tensor_scalar(T.k8s[:, :], T.k8o[:, :], (1.0, -1.0)[q], None, mult))
+            need("pe", t_ks, lb_free)
+            t_n = done("pe", PE.matmul(lb[:, 48:64], T.ones[:, 0:128], T.k8s[:, :], True, True))
+            need("v", t_n)
+            t = lb_free = done("v", V.tensor_reduce(cnt, lb[:, 48:64], AxisListType.X, add))
+            need("v", t)
+            t = done("v", V.tensor_scalar(t2b, t2, cnt, None, add))
+            ts2 = t2b
         need("v", t)
-        t = done("v", V.tensor_tensor(t3, t2, T.k8b[:, :], mult))
+        t = done("v", V.tensor_tensor(t3, ts2, T.k8b[:, :], mult))
         need("v", t, t_jt)
         t = done("v", V.tensor_tensor(t4, t3, jt, add))
         need("v", t)
         t_off = done("v", V.tensor_copy(T.off[:, :], t4))
-        need("v", t_val0)
-        t_val = done("v", V.tensor_scalar(T.val[:, :], T.val0[:, :], e0, e8, mult, add))
         need("v", t_off, t_val, t_sl0)
         t_sc = done("v", V.tensor_copy(T.sl[:, 0:SLW].indirect(T.off[:, 0:16]), T.val[:, :]))
         need("pe", t_sc, t_q)
@@ -241,21 +261,23 @@ def rank_program(g, core, T, topo):
                                         T.xr[:, 3:RES].indirect(T.lo[:, 64 * h + 32:64 * h + 64]), Copy))
             gath[h] = (tv, ts)
 
-        pass_on(0)
+        early(0)
         for h in halves:
             need("g", *gath[h])
             send([([dies[h][j]], T.pk[:, 1024 * h + 256 * j:1024 * h + 256 * j + 256], T["tk%d" % d][:, :], "tk%d" % d)
                   for j in range(4) if dies[h][j] != core], 4)
+        early(1)
         need("sy", *gath[halves[1]])
-        for k in range(1, PIECES):
-            load_piece("sy", k, 0)
-            load_piece("sy", k, 1)
+        for k in range(EARLY, PIECES):
+            load("sy", k, k + 1, 0, "w%d" % k)
+            load("sy", k, k + 1, 1, "w%d" % k)
+            piece[k][0] = piece[k][1]
             if k + 1 < PIECES:
-                need("sy", piece[k])
+                need("sy", piece[k][1])
 
         t_r1 = done("g", g.affine_select(T.r1[0:16, :], T.ones[0:16, 0:128], [[0, 8], [1, 16]], eq, 0.0, 0, -1))
         t_ut = done("g", g.affine_select(T.ut[0:16, :], T.ones[0:16, 0:128], [[0, 8], [1, 16]], ge, 0.0, 0, -1))
-        tt0, tt, rsc, rp, rc, rd, rf, rg, rh = [T.rr[:, 128 * i:128 * i + 128] for i in range(9)]
+        tt0, tt, rsc, rp, rc, rd, rf, rg, rh, rk = [T.rr[:, 128 * i:128 * i + 128] for i in range(10)]
         rs, ra, rb = [T.ri[:, 128 * i:128 * i + 128] for i in range(3)]
         t_tt = done("g", g.iota(tt0, [[16, 128]], 0, 0, allow_small_or_imprecise_dtypes=True))
         need("v", tki)
@@ -263,43 +285,18 @@ def rank_program(g, core, T, topo):
         tb = done("v", V.tensor_scalar(T.kin[0:16, :], T.ki[0:16, :], -1.0, None, mult))
         kp, kn = (T.kib, T.kin) if q == 0 else (T.kin, T.kib)
         need("pe", ta, tb, t_r1, t_ut, lb_free)
-        PE.matmul(T.lb[:, 0:128], T.r1[0:16, :], T.kib[0:16, :], True, True)
-        if d == 1:
-            PE.matmul(T.lb[:, 384:400], T.ones[:, 0:128], T.k8s[:, :], True, True)
-        PE.matmul(T.lb[:, 128:256], T.ones[0:16, 0:128], kp[0:16, :], True, True)
-        PE.matmul(T.lb[:, 256:384], T.ut[0:16, :], kp[0:16, :], True, False)
-        t_pe = done("pe", PE.matmul(T.lb[:, 256:384], T.ones[0:16, 0:128], kn[0:16, :], False, True))
-        need("v", t_tt)
-        t_t = done("v", V.tensor_scalar(tt, tt0, imf, None, add))
-        need("v", t_pe)
-        start = 0.0
-        if d == 1:
-            start = cnt
-            need("v", done("v", V.tensor_reduce(cnt, T.lb[:, 384:400], AxisListType.X, add)))
-        t = done("v", V.tensor_tensor_scan(rsc, T.onef[:, :], T.lb[:, 128:256], start, mult, add))
-        need("v", t)
-        t = done("v", V.tensor_tensor(rp, T.lb[:, 256:384], rsc, add))
-        need("v", t)
-        t = done("v", V.tensor_scalar(rs, rp, (-1.0, 2048.0)[q], None, add))
-        need("v", t)
-        t = done("v", V.tensor_scalar(ra, rs, 127, None, AluOpType.bitwise_and))
-        tb = done("v", V.tensor_scalar(rb, rs, 7, None, AluOpType.arith_shift_right))
-        need("v", t)
-        t = done("v", V.tensor_scalar(rc, ra, 16.0, 2048.0, mult, add))
-        need("v", t, tb)
-        t = done("v", V.tensor_tensor(rd, rc, rb, add))
-        need("v", t, t_t)
-        t = done("v", V.tensor_tensor(rf, rd, tt, sub))
-        need("v", t)
-        t = done("v", V.tensor_tensor(rg, T.lb[:, 0:128], rf, mult))
-        need("v", t)
-        t = done("v", V.tensor_tensor(rh, rg, tt, add))
-        need("v", t)
-        t_ro = done("v", V.tensor_copy(T.ro[:, :], rh))
+        PE.matmul(lb[:, 0:128], T.r1[0:16, :], T.kib[0:16, :], True, True)
+        PE.matmul(lb[:, 128:256], T.ones[0:16, 0:128], kp[0:16, :], True, True)
+        PE.matmul(lb[:, 256:384], T.ut[0:16, :], kp[0:16, :], True, False)
+        t_pe = done("pe", PE.matmul(lb[:, 256:384], T.ones[0:16, 0:128], kn[0:16, :], False, True))
     else:
         for k in range(PIECES):
-            piece[k] = expect("w%d" % k, 16)
-        pass_on(0)
+            if k < EARLY:
+                n = 4 if w == relay[k] else 16
+                piece[k] = [expect("w%d" % k, n), expect("v%d" % k, n)]
+            else:
+                piece[k] = [expect("w%d" % k, 16)] * 2
+        early(0)
 
     ca, cb = slice(128 * (1 - q), 128 * (1 - q) + 128), slice(128 * q, 128 * q + 128)
 
@@ -313,17 +310,50 @@ def rank_program(g, core, T, topo):
     need("g", t_xa)
     send([([across], T.xa[:, :], T.xc[:, :], "xc")], 1)
     if is_rank:
-        pass_on(1)
+        pass_on(EARLY)
+    else:
+        early(1)
     need("v", t_xb, expect("xc", len(engines([across]))))
     t_xm = done("v", V.tensor_tensor(T.xx[:, 0:128], T.xb[:, :], T.xc[:, :], add))
     need("g", t_xm)
     send([([partner], T.xx[:, 0:128], T.xx[:, 128:256], "xf")], 1)
     xready = (t_xm, expect("xf", 16))
-    for k in range(2 if is_rank else 1, PIECES):
+    for k in range(EARLY + 1 if is_rank else EARLY, PIECES):
         pass_on(k)
 
-    units = [(f, (0,)) for f in range(4)] + [(f, (1,)) for f in range(4)] + [(f, (0, 1)) for f in range(4, 10)] + \
-            [(f, (1,)) for f in range(10, 16)] + [(f, (0,)) for f in range(10, 16)]
+    if is_rank:
+        need("v", t_pe)
+        t = done("v", V.tensor_tensor_scan(rsc, T.onef[:, :], lb[:, 128:256], cnt if d == 1 else 0.0, mult, add))
+        t_k = done("v", V.tensor_copy(rk, lb[:, 0:128]))
+        need("v", t)
+        t = hb_free[NH - 1] = done("v", V.tensor_tensor(rp, lb[:, 256:384], rsc, add))
+        need("v", t_tt)
+        t_t = done("v", V.tensor_scalar(tt, tt0, imf, None, add))
+        need("v", t)
+        t = done("v", V.tensor_scalar(rs, rp, (-1.0, 2048.0)[q], None, add))
+        need("v", t)
+        t = done("v", V.tensor_scalar(ra, rs, 127, None, AluOpType.bitwise_and))
+        tb = done("v", V.tensor_scalar(rb, rs, 7, None, AluOpType.arith_shift_right))
+        need("v", t)
+        t = done("v", V.tensor_scalar(rc, ra, 16.0, 2048.0, mult, add))
+        need("v", t, tb)
+        t = done("v", V.tensor_tensor(rd, rc, rb, add))
+        need("v", t, t_t)
+        t = done("v", V.tensor_tensor(rf, rd, tt, sub))
+        need("v", t, t_k)
+        t = done("v", V.tensor_tensor(rg, rk, rf, mult))
+        need("v", t)
+        t = done("v", V.tensor_tensor(rh, rg, tt, add))
+        need("v", t)
+        t_ro = done("v", V.tensor_copy(T.ro[:, :], rh))
+
+    fs = list(range(NF))
+    if not is_rank:
+        a, b = CUTS[relay.index(w)], CUTS[relay.index(w) + 1]
+        fs = fs[a:b] + fs[:a] + fs[b:]
+    H0, H1, P = (0, 64, "yb0"), (64, 64, "yb2"), (128, 128, "yb1")
+    units = [(f, (H0, H1)) for f in fs[0:6]] + [(f, (P,)) for f in fs[0:6]] + [(f, (H0, H1, P)) for f in fs[6:8]] + \
+            [(f, (P,)) for f in fs[8:]] + [(f, (H0,)) for f in fs[8:]] + [(f, (H1,)) for f in fs[8:]]
     U = len(units)
     t_hr, t_l2 = [None] * U, [None] * U
     first, last = {}, {}
@@ -331,13 +361,19 @@ def rank_program(g, core, T, topo):
         for s in subs:
             first.setdefault(s, u)
             last[s] = u
+    t_yp = expect("yp", 16)
+    near, far = [r for r in ranks if r != core], chips[1 - q]
+    e_far = engines(far)
+    e_near = [e for e in engines(near) if e not in e_far]
+    t_y = None
     for step in range(U + LOOK):
         if step < U:
             u = step
             f, subs = units[u]
-            n, c0 = 128 * len(subs), 128 * subs[0]
+            n, c0 = sum(s[1] for s in subs), subs[0][0]
             hb, hr = T["hb%d" % (u % NH)], T["hr%d" % (u % NR)]
-            need("pe", hb_free[u % NH], piece[f // 4], *[xready[s] for s in subs])
+            k = [k for k in range(PIECES) if CUTS[k] <= f < CUTS[k + 1]][0]
+            need("pe", hb_free[u % NH], piece[k][0], xready[0] if H0 in subs else None, xready[1] if P in subs else None)
             t = done("pe", PE.matmul(hb[:, 0:n], T.wa[:, 128 * f:128 * f + 128], T.xx[:, c0:c0 + n], True, True))
             need("s", t, t_l2[u - NR] if u >= NR else None)
             t_hr[u] = hb_free[u % NH] = done("s", S.activation(hr[:, 0:n], hb[:, 0:n], Relu))
@@ -345,36 +381,42 @@ def rank_program(g, core, T, topo):
             u = step - LOOK
             f, subs = units[u]
             hr = T["hr%d" % (u % NR)]
-            need("pe", t_hr[u])
-            for i, s in enumerate(subs):
-                m = PE.matmul(T["yb%d" % s][:, 0:128], T.wb[:, 128 * f:128 * f + 128], hr[:, 128 * i:128 * i + 128],
-                              u == first[s], u == last[s])
+            k = [k for k in range(PIECES) if CUTS[k] <= f < CUTS[k + 1]][0]
+            need("pe", t_hr[u], piece[k][1])
+            for s in subs:
+                a = s[0] - subs[0][0]
+                m = PE.matmul(T[s[2]][:, 0:s[1]], T.wb[:, 128 * f:128 * f + 128], hr[:, a:a + s[1]], u == first[s], u == last[s])
             t_l2[u] = done("pe", m)
-            if u == last[1]:
+            for s in subs:
+                if u != last[s]:
+                    continue
                 need("v", t_l2[u])
-                t = done("v", V.tensor_copy(T.yo[:, :], T.yb1[:, 0:128]))
-                need("g", t)
-                send([([partner], T.yo[:, :], T.yp[:, :], "yp")], 1)
-    j0 = RES + 1024 * d + 256 * w + 128 * q
-    dst = T.xr[:, j0:j0 + 128]
-    src = dst if is_rank else T.ys[:, :]
-    need("v", t_l2[U - 1], expect("yp", 16))
-    t_y = done("v", V.tensor_tensor(src, T.yb0[:, 0:128], T.yp[:, :], add))
-    need("g", t_y)
-    near, far = [r for r in ranks if r != core], chips[1 - q]
-    e_far = engines(far)
-    fused([(far, src, dst, "res", e_far), (near, src, dst, "res", [e for e in engines(near) if e not in e_far])])
+                if s == P:
+                    t = done("v", V.tensor_copy(T.yo[:, :], T.yb1[:, 0:128]))
+                    need("g", t)
+                    send([([partner], T.yo[:, :], T.yp[:, :], "yp")], 1)
+                else:
+                    j0 = RES + 1024 * d + 256 * w + 128 * q + s[0]
+                    dst = T.xr[:, j0:j0 + 64]
+                    src = dst if is_rank else T.ys[:, s[0]:s[0] + 64]
+                    need("v", t_yp)
+                    t_y = done("v", V.tensor_tensor(src, T[s[2]][:, 0:64], T.yp[:, s[0]:s[0] + 64], add))
+                    need("g", t_y)
+                    fused([(far, src, dst, "res", e_far), (near, src, dst, "res", e_near)])
 
     if is_rank:
-        t_res = expect("res", 15 * 8)
+        t_res = expect("res", 15 * 2 * 8)
         need("v", t_res, t_ro, t_y)
-        tv = done("v", V.tensor_copy(T.yt[:, 0:1024], T.xr[:, 4:4100].indirect(T.ro[:, 0:64])))
         need("s", t_res, t_ro, t_y)
-        ts = done("s", S.activation(T.yt[:, 1024:2048], T.xr[:, 4:4100].indirect(T.ro[:, 64:128]), Copy))
-        need("sy", tv)
-        dma(g.sync.dma_start(T.y[:, 0:1024], T.yt[:, 0:1024]), "d_st")
-        need("s", ts)
-        dma(g.scalar.dma_start(T.y[:, 1024:2048], T.yt[:, 1024:2048]), "d_st")
+        for i in range(2):
+            cv, cs = slice(512 * i, 512 * i + 512), slice(1024 + 512 * i, 1536 + 512 * i)
+            tv = done("v", V.tensor_copy(T.yt[:, cv], T.xr[:, 4:4100].indirect(T.ro[:, 32 * i:32 * i + 32])))
+            ts = done("s", S.activation(T.yt[:, cs], T.xr[:, 4:4100].indirect(T.ro[:, 64 + 32 * i:96 + 32 * i]), Copy))
+            need("sy", tv)
+            dma(g.sync.dma_start(T.y[:, cv], T.yt[:, cv]), "d_st")
+            qn = ("sy", "s")[i]
+            need(qn, ts)
+            dma(queues[qn].dma_start(T.y[:, cs], T.yt[:, cs]), "d_st")
     for s in sorted(total):
         if seen.get(s, 0) < total[s]:
             need("g", (s, total[s]))

@@ -1,44 +1,50 @@
 from concourse.bass import DstId, RemoteDMATransfer
 from concourse.mybir import AluOpType, AxisListType, ActivationFunctionType
 
-NF = 16
-CUTS = (0, 2, 4, 6, 10, 13, 16)
-PIECES = 6
-EARLY = 3
-NH = 5
+NF = 8
+PIECES = 4
+TW = 256
+OFFS = (0, 192, 384, 576, 768, 896, 1024)
+NH = 4
 NR = 6
 LOOK = 4
-SLW = 2048 + 368
+SLW = 4096 + 368
 RES = 2052
+ARRIVE = {1: [(0, 4), (2, 4), (1, 16), (3, 16)], 2: [(1, 4), (0, 4), (2, 4), (3, 16)], 3: [(3, 4), (0, 4), (2, 4), (1, 16)],
+          4: [(0, 4), (1, 4), (2, 16), (3, 16)], 5: [(2, 4), (3, 4), (0, 16), (1, 16)]}
+DIRECT = {1: (0, 2), 2: (1,), 3: (3,), 4: (), 5: ()}
 
 SCRATCH = {
     "k8": ("sbuf", [128, 16], "int32"), "k8o": ("sbuf", [128, 16], "int32"), "k8s": ("sbuf", [128, 16], "bfloat16"),
     "k8b": ("sbuf", [128, 16], "bfloat16"), "k8n": ("sbuf", [128, 16], "bfloat16"),
     "ki": ("sbuf", [128, 128], "int32"), "kib": ("sbuf", [128, 128], "bfloat16"), "kin": ("sbuf", [128, 128], "bfloat16"),
-    "ones": ("sbuf", [128, 144], "bfloat16"), "onef": ("sbuf", [128, 128], "float32"),
+    "ones": ("sbuf", [128, 256], "bfloat16"), "onef": ("sbuf", [128, 128], "float32"),
     "mu": ("sbuf", [128, 128], "bfloat16"), "mb": ("sbuf", [128, 144], "bfloat16"),
     "r1": ("sbuf", [128, 128], "bfloat16"), "ut": ("sbuf", [128, 128], "bfloat16"),
     "ii": ("sbuf", [128, 4], "int32"),
     "ff": ("sbuf", [128, 8], "float32"),
     "q": ("sbuf", [128, 144], "bfloat16"), "val0": ("sbuf", [128, 256], "bfloat16"), "val": ("sbuf", [128, 256], "bfloat16"),
-    "ts": ("sbuf", [128, 128], "float32"),
+    "ts": ("sbuf", [128, 112], "float32"),
     "off": ("sbuf", [128, 16], "uint16"),
     "sl": ("sbuf", [128, SLW], "bfloat16"), "lo": ("sbuf", [128, 128], "uint16"), "ro": ("sbuf", [128, 128], "uint16"),
     "rr": ("sbuf", [128, 1280], "float32"), "ri": ("sbuf", [128, 384], "int32"),
     "xr": ("sbuf", [128, 4100], "float32"), "pk": ("sbuf", [128, 2048], "float32"), "yt": ("sbuf", [128, 2048], "float32"),
-    "wa": ("sbuf", [128, 2048], "float32"), "wb": ("sbuf", [128, 2048], "float32"),
-    "tk0": ("sbuf", [128, 256], "float32"), "tk1": ("sbuf", [128, 256], "float32"),
-    "xa": ("sbuf", [128, 128], "float32"), "xb": ("sbuf", [128, 128], "float32"), "xc": ("sbuf", [128, 128], "float32"),
-    "xx": ("sbuf", [128, 256], "float32"),
-    "yo": ("sbuf", [128, 128], "float32"), "yp": ("sbuf", [128, 128], "float32"), "ys": ("sbuf", [128, 128], "float32"),
-    "yb0": ("psum", [128, 512], "float32"), "yb1": ("psum", [128, 512], "float32"), "yb2": ("psum", [128, 512], "float32"),
+    "wa": ("sbuf", [128, 1024], "float32"), "wb": ("sbuf", [128, 1024], "float32"),
+    "tk0": ("sbuf", [128, 192], "float32"), "tk1": ("sbuf", [128, 192], "float32"),
+    "xa": ("sbuf", [128, 192], "float32"), "xc": ("sbuf", [128, 192], "float32"),
+    "xx": ("sbuf", [128, 384], "float32"),
+    "yo": ("sbuf", [128, 192], "float32"), "yp": ("sbuf", [128, 192], "float32"),
+    "sa": ("sbuf", [128, 192], "float32"), "sc": ("sbuf", [128, 192], "float32"), "ys": ("sbuf", [128, 192], "float32"),
+    "yb0": ("psum", [128, 512], "float32"), "yb1": ("psum", [128, 512], "float32"),
+    "yb2": ("psum", [128, 512], "float32"), "yb3": ("psum", [128, 512], "float32"),
 }
 for _i in range(NH):
     SCRATCH["hb%d" % _i] = ("psum", [128, 512], "float32")
 for _i in range(NR):
-    SCRATCH["hr%d" % _i] = ("sbuf", [128, 256], "float32")
-SEMAPHORES = ["c_pe", "c_v", "c_s", "c_g", "d_k8", "d_x", "d_ki", "d_st", "snd", "tk0", "tk1", "ko", "xc", "xf", "yp", "res"] + \
-    ["w%d" % k for k in range(PIECES)] + ["v%d" % k for k in range(EARLY)]
+    SCRATCH["hr%d" % _i] = ("sbuf", [128, 96], "float32")
+SEMAPHORES = ["c_pe", "c_v", "c_s", "c_g", "d_k8", "d_x", "d_ki", "d_st", "d_w1", "d_w2", "snd", "kos", "tk0", "tk1", "ko",
+              "xc0", "xc1", "xf0", "xf1", "yp0", "yp1", "sc0", "sc1", "res"] + \
+    ["w%d" % k for k in range(PIECES)] + ["v%d" % k for k in range(PIECES)]
 
 
 def rank_program(g, core, T, topo):
@@ -49,21 +55,31 @@ def rank_program(g, core, T, topo):
     for c in T.cores:
         if all(place(c) != place(rs[0]) for rs in chips):
             chips.append([r for r in T.cores if place(r) == place(c)])
-    here = [i for i in range(len(chips)) if place(chips[i][0]) == place(core)]
-    if not here:
+
+    def teams_of(rs):
+        mates = [c for c in range(256) if topo.mates(c, rs[0])]
+        chip = [c for c in range(256) if place(c) == place(rs[0])]
+        out = []
+        for r in rs:
+            helpers = [c for c in chip if topo.die(c) == topo.die(r) and c != r]
+            helpers.sort(key=lambda c: (not topo.may_write(c, mates[0]), c))
+            out.append([r] + helpers + [c for c in mates if topo.die(c) == topo.die(r) and topo.may_write(c, r)])
+        return out
+
+    teams = [teams_of(rs) for rs in chips]
+    found = [(i, j) for i in range(2) for j in range(2) if core in teams[i][j]]
+    if not found:
         return
-    q = here[0]
-
-    def dies_of(rs):
-        mine = [c for c in range(256) if place(c) == place(rs[0])]
-        return [[r] + [c for c in mine if topo.die(c) == topo.die(r) and c != r] for r in rs]
-
-    ranks, dies = chips[q], dies_of(chips[q])
-    d = [i for i in range(2) if core in dies[i]][0]
-    w = dies[d].index(core)
+    q, d = found[0]
+    ranks, team, other = chips[q], teams[q][d], teams[q][1 - d]
+    w = team.index(core)
     is_rank = w == 0
-    partner = dies[1 - d][w]
-    across = dies_of(chips[1 - q])[d][w]
+    is_mate = w > 3
+    partner = other[w]
+    across = teams[1 - q][d][w]
+    off_w = OFFS[w]
+    M = OFFS[w + 1] - off_w
+    Q = M // 2
 
     add, sub, mult = AluOpType.add, AluOpType.subtract, AluOpType.mult
     ge, eq = AluOpType.is_ge, AluOpType.is_equal
@@ -95,10 +111,10 @@ def rank_program(g, core, T, topo):
         inst.then_inc(T.sem[s], 16)
         return expect(s, 16)
 
-    def engines(dsts):
-        m = topo.mask(core, dsts[0])
+    def engines(dsts, src=core):
+        m = topo.mask(src, dsts[0])
         for c in dsts:
-            m &= topo.mask(core, c)
+            m &= topo.mask(src, c)
         return [1 << i for i in range(16) if (m >> i) & 1]
 
     def ids(dsts):
@@ -108,13 +124,13 @@ def rank_program(g, core, T, topo):
             out.append(DstId(rid=rid, pnc=pid))
         return out
 
-    def fused(items):
+    def fused(items, local="snd"):
         tr = []
         for dsts, src, dst, s, bits in items:
             tr.append(RemoteDMATransfer(dst_ids=ids(dsts), srcs=[src], dsts=[dst for _ in dsts],
                                         dma_engine_mask=sum(bits), remote_sem=T.sem[s]))
-            expect("snd", len(bits))
-        g.remote_dma_fused(tr, local_sem=T.sem["snd"])
+            expect(local, len(bits))
+        g.remote_dma_fused(tr, local_sem=T.sem[local])
 
     def send(items, n):
         full = []
@@ -124,77 +140,79 @@ def rank_program(g, core, T, topo):
             full.append(it + (e[j * k:(j + 1) * k],))
         fused(full)
 
-    relay = [1 + k % 3 for k in range(PIECES)]
-    piece = [[None, None] for _ in range(PIECES)]
+    offs = engines([across])
+    ons = [e for e in engines([partner]) if e not in offs]
 
-    def cols(k):
-        return slice(128 * CUTS[k], 128 * CUTS[k + 1])
+    piece = [[None] * PIECES, [None] * PIECES]
+    h1, h2, h3, m0, m1 = team[1:]
+    order = [0, 1, 2, 3] if is_rank else [k for k, n in ARRIVE[w]]
 
-    def others(k):
-        return [dies[d][j] for j in (1, 2, 3) if j != relay[k]]
+    def item(which, dsts, k):
+        cut = (T.wa, T.wb)[which][:, TW * k:TW * k + TW]
+        return (dsts, cut, cut, ("w%d", "v%d")[which] % k)
 
-    def early(which):
-        wt, nm = ((T.wa, "w%d"), (T.wb, "v%d"))[which]
+    def weights(which):
         if is_rank:
-            need("g", piece[0][which])
-            send([([dies[d][relay[k]]], wt[:, cols(k)], wt[:, cols(k)], nm % k) for k in range(EARLY)], 4)
+            need("g", piece[which][0])
+            e, n = ((offs + ons, 4), (ons, 2))[which]
+            fused([item(which, [c], k) + (e[n * k:n * k + n],) for k, c in enumerate([h1, h2, h1, h3])])
+        elif w == 1:
+            need("g", piece[which][0], piece[which][2])
+            send([item(which, [m0], 0), item(which, [m1], 2)], 2)
+            fused([item(which, [h2, h3], 0) + (ons[0:4],), item(which, [h2, h3], 2) + (ons[4:8],)])
+            if which == 0:
+                need("g", piece[which][1], piece[which][3])
+                send([item(which, [m0], 1), item(which, [m1], 3)], 2)
         else:
-            k = relay.index(w)
-            need("g", piece[k][which])
-            send([(others(k), wt[:, cols(k)], wt[:, cols(k)], nm % k)], 1)
+            k = DIRECT[w][0]
+            need("g", piece[which][k])
+            send([item(which, [h1, h3] if w == 2 else [h1, h2], k)], 1)
 
-    def pass_on(k):
-        if is_rank or w == relay[k]:
-            dsts = [dies[d][relay[k]]] if is_rank else others(k)
-            need("g", *piece[k])
-            send([(dsts, T.wa[:, cols(k)], T.wa[:, cols(k)], "w%d" % k), (dsts, T.wb[:, cols(k)], T.wb[:, cols(k)], "w%d" % k)], 2)
+    def swap(which, i):
+        k = ARRIVE[w][i][0]
+        need("g", piece[which][k])
+        send([item(which, [m1 if w == 4 else m0], k)], 1)
 
     lists = {}
     hb_free = [None] * NH
     lb = T["hb%d" % (NH - 1)]
     if is_rank:
-        f0 = NF * d * 128
-
-        def load(qn, k0, k1, which, s):
-            src, dst = (T.w1, T.wa) if which == 0 else (T.w2, T.wb)
-            a, b = 128 * CUTS[k0], 128 * CUTS[k1]
-            tok = dma(queues[qn].dma_start(dst[:, a:b], src[:, f0 + a:f0 + b]), s)
-            for k in range(k0, k1):
-                piece[k][which] = tok
-
+        f0 = NF * (2 * q + d) * 128
         for i in range(8):
             qn = ("sy", "s")[i % 2]
             tk8 = dma(queues[qn].dma_start(T.k8[16 * i:16 * i + 16, :], T.keep[:, 16 * i:16 * i + 16]), "d_k8")
-        load("s", 0, EARLY, 0, "w0")
-        tx = dma(g.sync.dma_start(T.xr[:, 4:RES], T.x[:, :]), "d_x")
-        tki = dma(g.sync.dma_start(T.ki[0:16, :], T.keep[:, :]), "d_ki")
-        load("sy", 0, EARLY, 1, "v0")
+        piece[0] = [dma(g.scalar.dma_start(T.wa[:, :], T.w1[:, f0:f0 + 1024]), "d_w1")] * PIECES
+        dma(g.sync.dma_start(T.xr[:, 4:1028], T.x[:, 0:1024]), "d_x")
 
         idx, im, gm = [T.ii[:, i:i + 1] for i in range(3)]
         e0, e8, g256, w8, wt, imf, base, cnt = [T.ff[:, i:i + 1] for i in range(8)]
-        jt, dj, sc, t1, t2, t2b, t3, t4 = [T.ts[:, 16 * i:16 * i + 16] for i in range(8)]
+        jt, dj, sc, t1, t2, t3, t4 = [T.ts[:, 16 * i:16 * i + 16] for i in range(7)]
         t_ones = done("v", V.memset(T.ones[:, :], 1.0))
         t_idx = done("g", g.iota(idx, [[1, 1]], 0, 1))
         need("g", t_ones)
-        t_mb = done("g", g.affine_select(T.mb[:, :], T.ones[:, :], [[16, 9], [0, 16]], ge, 0.0, -1, -1))
+        t_mb = done("g", g.affine_select(T.mb[:, :], T.ones[:, 0:144], [[16, 9], [0, 16]], ge, 0.0, -1, -1))
         t_mu = done("g", g.affine_select(T.mu[:, :], T.ones[:, 0:128], [[1, 128]], ge, 0.0, 0, -1))
-        t_jt = done("g", g.iota(jt, [[16, 16]], 2048, 1, allow_small_or_imprecise_dtypes=True))
+        t_jt = done("g", g.iota(jt, [[16, 16]], 2048 + 2048 * q, 1, allow_small_or_imprecise_dtypes=True))
         mb, me = T.mb[:, 0:128], T.mb[:, 16:144]
         if d == 0:
             need("g", tk8)
-            fused([([partner], T.k8[:, :], T.k8o[:, :], "ko", engines([partner])[0:8])])
+            fused([([partner], T.k8[:, :], T.k8o[:, :], "ko", engines([partner])[0:8])], "kos")
+            need("sy", ("kos", 8))
+        tx = dma(g.sync.dma_start(T.xr[:, 1028:RES], T.x[:, 1024:2048]), "d_x")
+        tki = dma(g.sync.dma_start(T.ki[0:16, :], T.keep[:, :]), "d_ki")
+        piece[1] = [dma(g.sync.dma_start(T.wb[:, :], T.w2[:, f0:f0 + 1024]), "d_w2")] * PIECES
         t_val0 = done("g", g.iota(T.val0[:, :], [[1, 256]], 1, 0, allow_small_or_imprecise_dtypes=True))
         done("v", V.memset(T.onef[:, :], 1.0))
-        t_z = done("v", V.memset(T.xr[:, 0:4], 0.0))
         done("v", V.memset(T.q[:, :], 0.0))
-        t_sl0 = done("v", V.memset(T.sl[:, :], 0.0))
+        need("s", t_ones)
+        for i in range(8):
+            t_sl0 = done("s", S.activation(T.sl[:, 256 * i:256 * i + 256], T.ones[:, :], Copy, scale=0.0))
         need("v", t_idx)
         done("v", V.tensor_scalar(im, idx, 15, None, AluOpType.bitwise_and))
         t = done("v", V.tensor_scalar(gm, idx, 4, None, AluOpType.arith_shift_right))
         need("v", t)
         done("v", V.tensor_scalar(e0, im, 0, None, eq))
         done("v", V.tensor_scalar(e8, im, 8, None, eq))
-        done("v", V.tensor_copy(imf, im))
         t = done("v", V.tensor_scalar(g256, gm, 256, None, mult))
         need("v", t)
         t = done("v", V.tensor_tensor(w8, g256, e8, mult))
@@ -207,6 +225,8 @@ def rank_program(g, core, T, topo):
         need("v", tk8)
         t_kb = done("v", V.tensor_copy(T.k8b[:, :], T.k8[:, :]))
         t_kn = done("v", V.tensor_scalar(T.k8n[:, :], T.k8[:, :], -1.0, None, mult))
+        done("v", V.tensor_copy(imf, im))
+        t_z = done("v", V.memset(T.xr[:, 0:4], 0.0))
         kp, kn = (T.k8b, T.k8n) if q == 0 else (T.k8n, T.k8b)
         need("pe", t_kb, t_kn, t_mb, t_mu)
         PE.matmul(lb[:, 0:16], me, kp[:, :], True, False)
@@ -224,8 +244,14 @@ def rank_program(g, core, T, topo):
         t = done("v", V.tensor_tensor(t2, t1, dj, add))
         need("v", t_val0)
         t_val = done("v", V.tensor_scalar(T.val[:, :], T.val0[:, :], e0, e8, mult, add))
-        ts2 = t2
-        if d == 1:
+        need("v", t)
+        t = done("v", V.tensor_tensor(t3, t2, T.k8b[:, :], mult))
+        need("v", t, t_jt)
+        t = done("v", V.tensor_tensor(t4, t3, jt, add))
+        if d == 0:
+            need("v", t)
+            t_off = done("v", V.tensor_copy(T.off[:, :], t4))
+        else:
             need("v", expect("ko", 8))
             t_ks = done("v", V.tensor_scalar(T.k8s[:, :], T.k8o[:, :], (1.0, -1.0)[q], None, mult))
             need("pe", t_ks, lb_free)
@@ -233,14 +259,7 @@ def rank_program(g, core, T, topo):
             need("v", t_n)
             t = lb_free = done("v", V.tensor_reduce(cnt, lb[:, 48:64], AxisListType.X, add))
             need("v", t)
-            t = done("v", V.tensor_scalar(t2b, t2, cnt, None, add))
-            ts2 = t2b
-        need("v", t)
-        t = done("v", V.tensor_tensor(t3, ts2, T.k8b[:, :], mult))
-        need("v", t, t_jt)
-        t = done("v", V.tensor_tensor(t4, t3, jt, add))
-        need("v", t)
-        t_off = done("v", V.tensor_copy(T.off[:, :], t4))
+            t_off = done("v", V.tensor_scalar(T.off[:, :], t4, cnt, None, add))
         need("v", t_off, t_val, t_sl0)
         t_sc = done("v", V.tensor_copy(T.sl[:, 0:SLW].indirect(T.off[:, 0:16]), T.val[:, :]))
         need("pe", t_sc, t_q)
@@ -261,19 +280,17 @@ def rank_program(g, core, T, topo):
                                         T.xr[:, 3:RES].indirect(T.lo[:, 64 * h + 32:64 * h + 64]), Copy))
             gath[h] = (tv, ts)
 
-        early(0)
+        weights(0)
         for h in halves:
             need("g", *gath[h])
-            send([([dies[h][j]], T.pk[:, 1024 * h + 256 * j:1024 * h + 256 * j + 256], T["tk%d" % d][:, :], "tk%d" % d)
-                  for j in range(4) if dies[h][j] != core], 4)
-        early(1)
-        need("sy", *gath[halves[1]])
-        for k in range(EARLY, PIECES):
-            load("sy", k, k + 1, 0, "w%d" % k)
-            load("sy", k, k + 1, 1, "w%d" % k)
-            piece[k][0] = piece[k][1]
-            if k + 1 < PIECES:
-                need("sy", piece[k][1])
+            for js, e, n in (((4, 5), offs, 4), ((0, 1, 2, 3), ons, 2)):
+                items = []
+                for j in js:
+                    c, a, b = teams[q][h][j], 1024 * h + OFFS[j], 1024 * h + OFFS[j + 1]
+                    if c != core:
+                        items.append(([c], T.pk[:, a:b], T["tk%d" % d][:, 0:b - a], "tk%d" % d))
+                fused([it + (e[n * i:n * i + n],) for i, it in enumerate(items)])
+        weights(1)
 
         t_r1 = done("g", g.affine_select(T.r1[0:16, :], T.ones[0:16, 0:128], [[0, 8], [1, 16]], eq, 0.0, 0, -1))
         t_ut = done("g", g.affine_select(T.ut[0:16, :], T.ones[0:16, 0:128], [[0, 8], [1, 16]], ge, 0.0, 0, -1))
@@ -290,36 +307,46 @@ def rank_program(g, core, T, topo):
         PE.matmul(lb[:, 256:384], T.ut[0:16, :], kp[0:16, :], True, False)
         t_pe = done("pe", PE.matmul(lb[:, 256:384], T.ones[0:16, 0:128], kn[0:16, :], False, True))
     else:
-        for k in range(PIECES):
-            if k < EARLY:
-                n = 4 if w == relay[k] else 16
-                piece[k] = [expect("w%d" % k, n), expect("v%d" % k, n)]
-            else:
-                piece[k] = [expect("w%d" % k, 16)] * 2
-        early(0)
+        for k, n in ARRIVE[w]:
+            piece[0][k] = expect("w%d" % k, n)
+            piece[1][k] = expect("v%d" % k, 2 if k in DIRECT[w] else n)
+        if is_mate:
+            swap(0, 0)
+        else:
+            weights(0)
 
-    ca, cb = slice(128 * (1 - q), 128 * (1 - q) + 128), slice(128 * q, 128 * q + 128)
+    def chunk(j):
+        return slice(Q * j, Q * j + Q)
 
-    def part(r, c):
-        return T.pk[:, 1024 * d + c.start:1024 * d + c.stop] if is_rank and r == d else T["tk%d" % r][:, c]
+    def part(r, j):
+        if is_rank and r == d:
+            a = 1024 * d + off_w + Q * j
+            return T.pk[:, a:a + Q]
+        return T["tk%d" % r][:, chunk(j)]
 
-    deps = list(gath[d]) if is_rank else [expect("tk%d" % d, 4)]
-    need("v", expect("tk%d" % (1 - d), 4), *deps)
-    t_xa = done("v", V.tensor_tensor(T.xa[:, :], part(0, ca), part(1, ca), add))
-    t_xb = done("v", V.tensor_tensor(T.xb[:, :], part(0, cb), part(1, cb), add))
-    need("g", t_xa)
-    send([([across], T.xa[:, :], T.xc[:, :], "xc")], 1)
+    n = 4 if is_mate else 2
+    deps = list(gath[d]) if is_rank else [expect("tk%d" % d, n)]
+    need("v", expect("tk%d" % (1 - d), n), *deps)
+    t_xa = [done("v", V.tensor_tensor(T.xa[:, chunk(j)], part(0, j), part(1, j), add)) for j in range(2)]
+    for j in range(2):
+        need("g", t_xa[j])
+        send([([across], T.xa[:, chunk(j)], T.xc[:, chunk(j)], "xc%d" % j)], 1)
     if is_rank:
-        pass_on(EARLY)
+        send([item(1, [m0], 1), item(1, [m1], 3)], 2)
+    elif is_mate:
+        swap(0, 1)
     else:
-        early(1)
-    need("v", t_xb, expect("xc", len(engines([across]))))
-    t_xm = done("v", V.tensor_tensor(T.xx[:, 0:128], T.xb[:, :], T.xc[:, :], add))
-    need("g", t_xm)
-    send([([partner], T.xx[:, 0:128], T.xx[:, 128:256], "xf")], 1)
-    xready = (t_xm, expect("xf", 16))
-    for k in range(EARLY + 1 if is_rank else EARLY, PIECES):
-        pass_on(k)
+        weights(1)
+    t_xm, t_xf = [None, None], [None, None]
+    for j in range(2):
+        need("v", t_xa[j], expect("xc%d" % j, len(engines([core], across))))
+        t_xm[j] = done("v", V.tensor_tensor(T.xx[:, chunk(j)], T.xa[:, chunk(j)], T.xc[:, chunk(j)], add))
+        need("g", t_xm[j])
+        send([([partner], T.xx[:, chunk(j)], T.xx[:, M + Q * j:M + Q * j + Q], "xf%d" % j)], 1)
+        t_xf[j] = expect("xf%d" % j, len(engines([core], partner)))
+    if is_mate:
+        swap(1, 0)
+        swap(1, 1)
 
     if is_rank:
         need("v", t_pe)
@@ -347,67 +374,73 @@ def rank_program(g, core, T, topo):
         need("v", t)
         t_ro = done("v", V.tensor_copy(T.ro[:, :], rh))
 
-    fs = list(range(NF))
-    if not is_rank:
-        a, b = CUTS[relay.index(w)], CUTS[relay.index(w) + 1]
-        fs = fs[a:b] + fs[:a] + fs[b:]
-    H0, H1, P = (0, 64, "yb0"), (64, 64, "yb2"), (128, 128, "yb1")
-    units = [(f, (H0, H1)) for f in fs[0:6]] + [(f, (P,)) for f in fs[0:6]] + [(f, (H0, H1, P)) for f in fs[6:8]] + \
-            [(f, (P,)) for f in fs[8:]] + [(f, (H0,)) for f in fs[8:]] + [(f, (H1,)) for f in fs[8:]]
+    fs = [2 * k + i for k in order for i in range(2)]
+    H0, H1, P0, P1 = range(4)
+    ready = t_xm + t_xf
+    units = [(f, H0) for f in fs[0:2]] + [(f, H1) for f in fs[0:2]] + [(f, H0) for f in fs[2:]] + \
+            [(f, P0) for f in fs] + [(f, P1) for f in fs] + [(f, H1) for f in fs[2:]]
     U = len(units)
     t_hr, t_l2 = [None] * U, [None] * U
     first, last = {}, {}
-    for u, (f, subs) in enumerate(units):
-        for s in subs:
-            first.setdefault(s, u)
-            last[s] = u
-    t_yp = expect("yp", 16)
-    near, far = [r for r in ranks if r != core], chips[1 - q]
-    e_far = engines(far)
-    e_near = [e for e in engines(near) if e not in e_far]
-    t_y = None
+    for u, (f, s) in enumerate(units):
+        first.setdefault(s, u)
+        last[s] = u
+    near = [r for r in ranks if r != core]
+    t_yp = [expect("yp%d" % j, len(engines([core], partner))) for j in range(2)]
+    t_sc = [expect("sc%d" % j, len(engines([core], across))) for j in range(2)]
+    t_sa, t_y = [None, None], [None, None]
+
+    def give(j):
+        need("v", t_l2[last[P0 + j]])
+        t = done("v", V.tensor_copy(T.yo[:, chunk(j)], T["yb%d" % (P0 + j)][:, 0:Q]))
+        need("g", t)
+        send([([partner], T.yo[:, chunk(j)], T.yp[:, chunk(j)], "yp%d" % j)], 1)
+
+    def cross(j):
+        need("v", t_l2[last[j]], t_yp[j])
+        t_sa[j] = done("v", V.tensor_tensor(T.sa[:, chunk(j)], T["yb%d" % j][:, 0:Q], T.yp[:, chunk(j)], add))
+        need("g", t_sa[j])
+        send([([across], T.sa[:, chunk(j)], T.sc[:, chunk(j)], "sc%d" % j)], 1)
+
+    def deliver(j):
+        j0 = RES + 1024 * d + off_w + Q * j
+        dst = T.xr[:, j0:j0 + Q]
+        src = dst if is_rank else T.ys[:, chunk(j)]
+        need("v", t_sa[j], t_sc[j])
+        t_y[j] = done("v", V.tensor_tensor(src, T.sa[:, chunk(j)], T.sc[:, chunk(j)], add))
+        need("g", t_y[j])
+        send([(near, src, dst, "res")], 1)
+
     for step in range(U + LOOK):
         if step < U:
             u = step
-            f, subs = units[u]
-            n, c0 = sum(s[1] for s in subs), subs[0][0]
+            f, s = units[u]
             hb, hr = T["hb%d" % (u % NH)], T["hr%d" % (u % NR)]
-            k = [k for k in range(PIECES) if CUTS[k] <= f < CUTS[k + 1]][0]
-            need("pe", hb_free[u % NH], piece[k][0], xready[0] if H0 in subs else None, xready[1] if P in subs else None)
-            t = done("pe", PE.matmul(hb[:, 0:n], T.wa[:, 128 * f:128 * f + 128], T.xx[:, c0:c0 + n], True, True))
+            need("pe", hb_free[u % NH], piece[0][f // 2], ready[s])
+            t = done("pe", PE.matmul(hb[:, 0:Q], T.wa[:, 128 * f:128 * f + 128], T.xx[:, Q * s:Q * s + Q], True, True))
             need("s", t, t_l2[u - NR] if u >= NR else None)
-            t_hr[u] = hb_free[u % NH] = done("s", S.activation(hr[:, 0:n], hb[:, 0:n], Relu))
+            t_hr[u] = hb_free[u % NH] = done("s", S.activation(hr[:, 0:Q], hb[:, 0:Q], Relu))
         if step >= LOOK:
             u = step - LOOK
-            f, subs = units[u]
+            f, s = units[u]
             hr = T["hr%d" % (u % NR)]
-            k = [k for k in range(PIECES) if CUTS[k] <= f < CUTS[k + 1]][0]
-            need("pe", t_hr[u], piece[k][1])
-            for s in subs:
-                a = s[0] - subs[0][0]
-                m = PE.matmul(T[s[2]][:, 0:s[1]], T.wb[:, 128 * f:128 * f + 128], hr[:, a:a + s[1]], u == first[s], u == last[s])
+            need("pe", t_hr[u], piece[1][f // 2])
+            m = PE.matmul(T["yb%d" % s][:, 0:Q], T.wb[:, 128 * f:128 * f + 128], hr[:, 0:Q], u == first[s], u == last[s])
             t_l2[u] = done("pe", m)
-            for s in subs:
-                if u != last[s]:
-                    continue
-                need("v", t_l2[u])
-                if s == P:
-                    t = done("v", V.tensor_copy(T.yo[:, :], T.yb1[:, 0:128]))
-                    need("g", t)
-                    send([([partner], T.yo[:, :], T.yp[:, :], "yp")], 1)
-                else:
-                    j0 = RES + 1024 * d + 256 * w + 128 * q + s[0]
-                    dst = T.xr[:, j0:j0 + 64]
-                    src = dst if is_rank else T.ys[:, s[0]:s[0] + 64]
-                    need("v", t_yp)
-                    t_y = done("v", V.tensor_tensor(src, T[s[2]][:, 0:64], T.yp[:, s[0]:s[0] + 64], add))
-                    need("g", t_y)
-                    fused([(far, src, dst, "res", e_far), (near, src, dst, "res", e_near)])
+            if u == last[P0]:
+                give(0)
+                cross(0)
+            if u == last[P1]:
+                give(1)
+    cross(1)
+    deliver(0)
+    deliver(1)
 
     if is_rank:
-        t_res = expect("res", 15 * 2 * 8)
-        need("v", t_res, t_ro, t_y)
-        need("s", t_res, t_ro, t_y)
+        n = sum(2 * len(engines([core], c)) for tm in teams[q] for c in tm if c != core)
+        t_res = expect("res", n)
+        need("v", t_res, t_ro, *t_y)
+        need("s", t_res, t_ro, *t_y)
         for i in range(2):
             cv, cs = slice(512 * i, 512 * i + 512), slice(1024 + 512 * i, 1536 + 512 * i)
             tv = done("v", V.tensor_copy(T.yt[:, cv], T.xr[:, 4:4100].indirect(T.ro[:, 32 * i:32 * i + 32])))

from concourse.bass import DstId, RemoteDMATransfer
from concourse.mybir import AluOpType, AxisListType, ActivationFunctionType

NF = 8
PIECES = 4
TW = 256
OFFS = (0, 192, 384, 576, 768, 896, 1024)
NH = 4
NR = 6
LOOK = 4
SLW = 4096 + 368
RES = 2052
ARRIVE = {1: [(0, 4), (2, 4), (1, 16), (3, 16)], 2: [(1, 4), (0, 4), (2, 4), (3, 16)], 3: [(3, 4), (0, 4), (2, 4), (1, 16)],
          4: [(0, 4), (1, 4), (2, 16), (3, 16)], 5: [(2, 4), (3, 4), (0, 16), (1, 16)]}
DIRECT = {1: (0, 2), 2: (1,), 3: (3,), 4: (), 5: ()}

SCRATCH = {
    "k8": ("sbuf", [128, 16], "int32"), "k8o": ("sbuf", [128, 16], "int32"), "k8s": ("sbuf", [128, 16], "bfloat16"),
    "k8b": ("sbuf", [128, 16], "bfloat16"), "k8n": ("sbuf", [128, 16], "bfloat16"),
    "ki": ("sbuf", [128, 128], "int32"), "kib": ("sbuf", [128, 128], "bfloat16"), "kin": ("sbuf", [128, 128], "bfloat16"),
    "ones": ("sbuf", [128, 256], "bfloat16"), "onef": ("sbuf", [128, 128], "float32"),
    "mu": ("sbuf", [128, 128], "bfloat16"), "mb": ("sbuf", [128, 144], "bfloat16"),
    "r1": ("sbuf", [128, 128], "bfloat16"), "ut": ("sbuf", [128, 128], "bfloat16"),
    "ii": ("sbuf", [128, 4], "int32"),
    "ff": ("sbuf", [128, 8], "float32"),
    "q": ("sbuf", [128, 144], "bfloat16"), "val0": ("sbuf", [128, 256], "bfloat16"), "val": ("sbuf", [128, 256], "bfloat16"),
    "ts": ("sbuf", [128, 112], "float32"),
    "off": ("sbuf", [128, 16], "uint16"),
    "sl": ("sbuf", [128, SLW], "bfloat16"), "lo": ("sbuf", [128, 128], "uint16"), "ro": ("sbuf", [128, 128], "uint16"),
    "rr": ("sbuf", [128, 1280], "float32"), "ri": ("sbuf", [128, 384], "int32"),
    "xr": ("sbuf", [128, 4100], "float32"), "pk": ("sbuf", [128, 2048], "float32"), "yt": ("sbuf", [128, 2048], "float32"),
    "wa": ("sbuf", [128, 1024], "float32"), "wb": ("sbuf", [128, 1024], "float32"),
    "tk0": ("sbuf", [128, 192], "float32"), "tk1": ("sbuf", [128, 192], "float32"),
    "xa": ("sbuf", [128, 192], "float32"), "xc": ("sbuf", [128, 192], "float32"),
    "xx": ("sbuf", [128, 384], "float32"),
    "yo": ("sbuf", [128, 192], "float32"), "yp": ("sbuf", [128, 192], "float32"),
    "sa": ("sbuf", [128, 192], "float32"), "sc": ("sbuf", [128, 192], "float32"), "ys": ("sbuf", [128, 192], "float32"),
    "yb0": ("psum", [128, 512], "float32"), "yb1": ("psum", [128, 512], "float32"),
    "yb2": ("psum", [128, 512], "float32"), "yb3": ("psum", [128, 512], "float32"),
}
for _i in range(NH):
    SCRATCH["hb%d" % _i] = ("psum", [128, 512], "float32")
for _i in range(NR):
    SCRATCH["hr%d" % _i] = ("sbuf", [128, 96], "float32")
SEMAPHORES = ["c_pe", "c_v", "c_s", "c_g", "d_k8", "d_x", "d_ki", "d_st", "d_w1", "d_w2", "snd", "kos", "tk0", "tk1", "ko",
              "xc0", "xc1", "xf0", "xf1", "yp0", "yp1", "sc0", "sc1", "res"] + \
    ["w%d" % k for k in range(PIECES)] + ["v%d" % k for k in range(PIECES)]


def rank_program(g, core, T, topo):
    def place(c):
        return (topo.host(c), topo.chip(c))

    chips = []
    for c in T.cores:
        if all(place(c) != place(rs[0]) for rs in chips):
            chips.append([r for r in T.cores if place(r) == place(c)])

    def teams_of(rs):
        mates = [c for c in range(256) if topo.mates(c, rs[0])]
        chip = [c for c in range(256) if place(c) == place(rs[0])]
        out = []
        for r in rs:
            helpers = [c for c in chip if topo.die(c) == topo.die(r) and c != r]
            helpers.sort(key=lambda c: (not topo.may_write(c, mates[0]), c))
            out.append([r] + helpers + [c for c in mates if topo.die(c) == topo.die(r) and topo.may_write(c, r)])
        return out

    teams = [teams_of(rs) for rs in chips]
    found = [(i, j) for i in range(2) for j in range(2) if core in teams[i][j]]
    if not found:
        return
    q, d = found[0]
    ranks, team, other = chips[q], teams[q][d], teams[q][1 - d]
    w = team.index(core)
    is_rank = w == 0
    is_mate = w > 3
    partner = other[w]
    across = teams[1 - q][d][w]
    off_w = OFFS[w]
    M = OFFS[w + 1] - off_w
    Q = M // 2

    add, sub, mult = AluOpType.add, AluOpType.subtract, AluOpType.mult
    ge, eq = AluOpType.is_ge, AluOpType.is_equal
    Copy, Relu = ActivationFunctionType.Copy, ActivationFunctionType.Relu
    V, S, PE = g.vector, g.scalar, g.tensor
    queues = {"pe": g.tensor, "v": g.vector, "s": g.scalar, "g": g, "sy": g.sync}
    total, waited, seen = {}, {}, {}

    def need(qn, *deps):
        best = {}
        for dep in deps:
            if dep is not None:
                best[dep[0]] = max(best.get(dep[0], 0), dep[1])
        for s, v in best.items():
            if waited.get((qn, s), 0) < v:
                queues[qn].wait_ge(T.sem[s], v)
                waited[(qn, s)] = v
                seen[s] = max(seen.get(s, 0), v)

    def expect(s, n):
        total[s] = total.get(s, 0) + n
        return (s, total[s])

    def done(qn, inst):
        inst.then_inc(T.sem["c_" + qn], 1)
        return expect("c_" + qn, 1)

    def dma(inst, s):
        inst.then_inc(T.sem[s], 16)
        return expect(s, 16)

    def engines(dsts, src=core):
        m = topo.mask(src, dsts[0])
        for c in dsts:
            m &= topo.mask(src, c)
        return [1 << i for i in range(16) if (m >> i) & 1]

    def ids(dsts):
        out = []
        for c in dsts:
            rid, pid = topo.addr(c, core)
            out.append(DstId(rid=rid, pnc=pid))
        return out

    def fused(items, local="snd"):
        tr = []
        for dsts, src, dst, s, bits in items:
            tr.append(RemoteDMATransfer(dst_ids=ids(dsts), srcs=[src], dsts=[dst for _ in dsts],
                                        dma_engine_mask=sum(bits), remote_sem=T.sem[s]))
            expect(local, len(bits))
        g.remote_dma_fused(tr, local_sem=T.sem[local])

    def send(items, n):
        full = []
        for j, it in enumerate(items):
            e = engines(it[0])
            k = len(e) // n
            full.append(it + (e[j * k:(j + 1) * k],))
        fused(full)

    offs = engines([across])
    ons = [e for e in engines([partner]) if e not in offs]

    piece = [[None] * PIECES, [None] * PIECES]
    h1, h2, h3, m0, m1 = team[1:]
    order = [0, 1, 2, 3] if is_rank else [k for k, n in ARRIVE[w]]

    def item(which, dsts, k):
        cut = (T.wa, T.wb)[which][:, TW * k:TW * k + TW]
        return (dsts, cut, cut, ("w%d", "v%d")[which] % k)

    def weights(which):
        if is_rank:
            need("g", piece[which][0])
            e, n = ((offs + ons, 4), (ons, 2))[which]
            fused([item(which, [c], k) + (e[n * k:n * k + n],) for k, c in enumerate([h1, h2, h1, h3])])
        elif w == 1:
            need("g", piece[which][0], piece[which][2])
            send([item(which, [m0], 0), item(which, [m1], 2)], 2)
            fused([item(which, [h2, h3], 0) + (ons[0:4],), item(which, [h2, h3], 2) + (ons[4:8],)])
            if which == 0:
                need("g", piece[which][1], piece[which][3])
                send([item(which, [m0], 1), item(which, [m1], 3)], 2)
        else:
            k = DIRECT[w][0]
            need("g", piece[which][k])
            send([item(which, [h1, h3] if w == 2 else [h1, h2], k)], 1)

    def swap(which, i):
        k = ARRIVE[w][i][0]
        need("g", piece[which][k])
        send([item(which, [m1 if w == 4 else m0], k)], 1)

    lists = {}
    hb_free = [None] * NH
    lb = T["hb%d" % (NH - 1)]
    if is_rank:
        f0 = NF * (2 * q + d) * 128
        for i in range(8):
            qn = ("sy", "s")[i % 2]
            tk8 = dma(queues[qn].dma_start(T.k8[16 * i:16 * i + 16, :], T.keep[:, 16 * i:16 * i + 16]), "d_k8")
        piece[0] = [dma(g.scalar.dma_start(T.wa[:, :], T.w1[:, f0:f0 + 1024]), "d_w1")] * PIECES
        dma(g.sync.dma_start(T.xr[:, 4:1028], T.x[:, 0:1024]), "d_x")

        idx, im, gm = [T.ii[:, i:i + 1] for i in range(3)]
        e0, e8, g256, w8, wt, imf, base, cnt = [T.ff[:, i:i + 1] for i in range(8)]
        jt, dj, sc, t1, t2, t3, t4 = [T.ts[:, 16 * i:16 * i + 16] for i in range(7)]
        t_ones = done("v", V.memset(T.ones[:, :], 1.0))
        t_idx = done("g", g.iota(idx, [[1, 1]], 0, 1))
        need("g", t_ones)
        t_mb = done("g", g.affine_select(T.mb[:, :], T.ones[:, 0:144], [[16, 9], [0, 16]], ge, 0.0, -1, -1))
        t_mu = done("g", g.affine_select(T.mu[:, :], T.ones[:, 0:128], [[1, 128]], ge, 0.0, 0, -1))
        t_jt = done("g", g.iota(jt, [[16, 16]], 2048 + 2048 * q, 1, allow_small_or_imprecise_dtypes=True))
        mb, me = T.mb[:, 0:128], T.mb[:, 16:144]
        if d == 0:
            need("g", tk8)
            fused([([partner], T.k8[:, :], T.k8o[:, :], "ko", engines([partner])[0:8])], "kos")
            need("sy", ("kos", 8))
        tx = dma(g.sync.dma_start(T.xr[:, 1028:RES], T.x[:, 1024:2048]), "d_x")
        tki = dma(g.sync.dma_start(T.ki[0:16, :], T.keep[:, :]), "d_ki")
        piece[1] = [dma(g.sync.dma_start(T.wb[:, :], T.w2[:, f0:f0 + 1024]), "d_w2")] * PIECES
        t_val0 = done("g", g.iota(T.val0[:, :], [[1, 256]], 1, 0, allow_small_or_imprecise_dtypes=True))
        done("v", V.memset(T.onef[:, :], 1.0))
        done("v", V.memset(T.q[:, :], 0.0))
        need("s", t_ones)
        for i in range(8):
            t_sl0 = done("s", S.activation(T.sl[:, 256 * i:256 * i + 256], T.ones[:, :], Copy, scale=0.0))
        need("v", t_idx)
        done("v", V.tensor_scalar(im, idx, 15, None, AluOpType.bitwise_and))
        t = done("v", V.tensor_scalar(gm, idx, 4, None, AluOpType.arith_shift_right))
        need("v", t)
        done("v", V.tensor_scalar(e0, im, 0, None, eq))
        done("v", V.tensor_scalar(e8, im, 8, None, eq))
        t = done("v", V.tensor_scalar(g256, gm, 256, None, mult))
        need("v", t)
        t = done("v", V.tensor_tensor(w8, g256, e8, mult))
        need("v", t)
        t = done("v", V.tensor_tensor(wt, w8, e0, add))
        need("v", t, t_jt)
        t_dj = done("v", V.tensor_scalar(dj, jt, -1.0, (-1.0, 2048.0)[q], mult, add))
        t_q = done("v", V.tensor_scalar(T.q[:, 0:144:16], T.onef[:, 0:9], wt, None, mult))

        need("v", tk8)
        t_kb = done("v", V.tensor_copy(T.k8b[:, :], T.k8[:, :]))
        t_kn = done("v", V.tensor_scalar(T.k8n[:, :], T.k8[:, :], -1.0, None, mult))
        done("v", V.tensor_copy(imf, im))
        t_z = done("v", V.memset(T.xr[:, 0:4], 0.0))
        kp, kn = (T.k8b, T.k8n) if q == 0 else (T.k8n, T.k8b)
        need("pe", t_kb, t_kn, t_mb, t_mu)
        PE.matmul(lb[:, 0:16], me, kp[:, :], True, False)
        PE.matmul(lb[:, 0:16], mb, kn[:, :], False, True)
        PE.matmul(lb[:, 16:32], T.mu[:, :], kp[:, :], True, False)
        PE.matmul(lb[:, 16:32], me, kn[:, :], False, True)
        t_pre = done("pe", PE.matmul(lb[:, 32:48], mb, kp[:, :], True, True))
        need("v", t_pre)
        t = done("v", V.tensor_reduce(base, lb[:, 32:48], AxisListType.X, add))
        need("v", t)
        t = done("v", V.tensor_tensor_scan(sc, T.onef[:, 0:16], lb[:, 0:16], base, mult, add))
        need("v", t, t_dj)
        t = lb_free = done("v", V.tensor_tensor(t1, lb[:, 16:32], sc, add))
        need("v", t)
        t = done("v", V.tensor_tensor(t2, t1, dj, add))
        need("v", t_val0)
        t_val = done("v", V.tensor_scalar(T.val[:, :], T.val0[:, :], e0, e8, mult, add))
        need("v", t)
        t = done("v", V.tensor_tensor(t3, t2, T.k8b[:, :], mult))
        need("v", t, t_jt)
        t = done("v", V.tensor_tensor(t4, t3, jt, add))
        if d == 0:
            need("v", t)
            t_off = done("v", V.tensor_copy(T.off[:, :], t4))
        else:
            need("v", expect("ko", 8))
            t_ks = done("v", V.tensor_scalar(T.k8s[:, :], T.k8o[:, :], (1.0, -1.0)[q], None, mult))
            need("pe", t_ks, lb_free)
            t_n = done("pe", PE.matmul(lb[:, 48:64], T.ones[:, 0:128], T.k8s[:, :], True, True))
            need("v", t_n)
            t = lb_free = done("v", V.tensor_reduce(cnt, lb[:, 48:64], AxisListType.X, add))
            need("v", t)
            t_off = done("v", V.tensor_scalar(T.off[:, :], t4, cnt, None, add))
        need("v", t_off, t_val, t_sl0)
        t_sc = done("v", V.tensor_copy(T.sl[:, 0:SLW].indirect(T.off[:, 0:16]), T.val[:, :]))
        need("pe", t_sc, t_q)
        halves = [1 - d, d]
        for h in halves:
            for i in range(16):
                m = PE.matmul(T["hb%d" % h][:, 0:64], T.q[:, 16 - i:144 - i], T.sl[:, 128 * i + 64 * h:128 * i + 64 * h + 64],
                              i == 0, i == 15)
            lists[h] = done("pe", m)
        gath = {}
        for h in halves:
            need("v", lists[h])
            lists[h] = hb_free[h] = done("v", V.tensor_copy(T.lo[:, 64 * h:64 * h + 64], T["hb%d" % h][:, 0:64]))
            need("v", lists[h], tx, t_z)
            tv = done("v", V.tensor_copy(T.pk[:, 1024 * h:1024 * h + 512], T.xr[:, 3:RES].indirect(T.lo[:, 64 * h:64 * h + 32])))
            need("s", lists[h], tx, t_z)
            ts = done("s", S.activation(T.pk[:, 1024 * h + 512:1024 * h + 1024],
                                        T.xr[:, 3:RES].indirect(T.lo[:, 64 * h + 32:64 * h + 64]), Copy))
            gath[h] = (tv, ts)

        weights(0)
        for h in halves:
            need("g", *gath[h])
            for js, e, n in (((4, 5), offs, 4), ((0, 1, 2, 3), ons, 2)):
                items = []
                for j in js:
                    c, a, b = teams[q][h][j], 1024 * h + OFFS[j], 1024 * h + OFFS[j + 1]
                    if c != core:
                        items.append(([c], T.pk[:, a:b], T["tk%d" % d][:, 0:b - a], "tk%d" % d))
                fused([it + (e[n * i:n * i + n],) for i, it in enumerate(items)])
        weights(1)

        t_r1 = done("g", g.affine_select(T.r1[0:16, :], T.ones[0:16, 0:128], [[0, 8], [1, 16]], eq, 0.0, 0, -1))
        t_ut = done("g", g.affine_select(T.ut[0:16, :], T.ones[0:16, 0:128], [[0, 8], [1, 16]], ge, 0.0, 0, -1))
        tt0, tt, rsc, rp, rc, rd, rf, rg, rh, rk = [T.rr[:, 128 * i:128 * i + 128] for i in range(10)]
        rs, ra, rb = [T.ri[:, 128 * i:128 * i + 128] for i in range(3)]
        t_tt = done("g", g.iota(tt0, [[16, 128]], 0, 0, allow_small_or_imprecise_dtypes=True))
        need("v", tki)
        ta = done("v", V.tensor_copy(T.kib[0:16, :], T.ki[0:16, :]))
        tb = done("v", V.tensor_scalar(T.kin[0:16, :], T.ki[0:16, :], -1.0, None, mult))
        kp, kn = (T.kib, T.kin) if q == 0 else (T.kin, T.kib)
        need("pe", ta, tb, t_r1, t_ut, lb_free)
        PE.matmul(lb[:, 0:128], T.r1[0:16, :], T.kib[0:16, :], True, True)
        PE.matmul(lb[:, 128:256], T.ones[0:16, 0:128], kp[0:16, :], True, True)
        PE.matmul(lb[:, 256:384], T.ut[0:16, :], kp[0:16, :], True, False)
        t_pe = done("pe", PE.matmul(lb[:, 256:384], T.ones[0:16, 0:128], kn[0:16, :], False, True))
    else:
        for k, n in ARRIVE[w]:
            piece[0][k] = expect("w%d" % k, n)
            piece[1][k] = expect("v%d" % k, 2 if k in DIRECT[w] else n)
        if is_mate:
            swap(0, 0)
        else:
            weights(0)

    def chunk(j):
        return slice(Q * j, Q * j + Q)

    def part(r, j):
        if is_rank and r == d:
            a = 1024 * d + off_w + Q * j
            return T.pk[:, a:a + Q]
        return T["tk%d" % r][:, chunk(j)]

    n = 4 if is_mate else 2
    deps = list(gath[d]) if is_rank else [expect("tk%d" % d, n)]
    need("v", expect("tk%d" % (1 - d), n), *deps)
    t_xa = [done("v", V.tensor_tensor(T.xa[:, chunk(j)], part(0, j), part(1, j), add)) for j in range(2)]
    for j in range(2):
        need("g", t_xa[j])
        send([([across], T.xa[:, chunk(j)], T.xc[:, chunk(j)], "xc%d" % j)], 1)
    if is_rank:
        send([item(1, [m0], 1), item(1, [m1], 3)], 2)
    elif is_mate:
        swap(0, 1)
    else:
        weights(1)
    t_xm, t_xf = [None, None], [None, None]
    for j in range(2):
        need("v", t_xa[j], expect("xc%d" % j, len(engines([core], across))))
        t_xm[j] = done("v", V.tensor_tensor(T.xx[:, chunk(j)], T.xa[:, chunk(j)], T.xc[:, chunk(j)], add))
        need("g", t_xm[j])
        send([([partner], T.xx[:, chunk(j)], T.xx[:, M + Q * j:M + Q * j + Q], "xf%d" % j)], 1)
        t_xf[j] = expect("xf%d" % j, len(engines([core], partner)))
    if is_mate:
        swap(1, 0)
        swap(1, 1)

    if is_rank:
        need("v", t_pe)
        t = done("v", V.tensor_tensor_scan(rsc, T.onef[:, :], lb[:, 128:256], cnt if d == 1 else 0.0, mult, add))
        t_k = done("v", V.tensor_copy(rk, lb[:, 0:128]))
        need("v", t)
        t = hb_free[NH - 1] = done("v", V.tensor_tensor(rp, lb[:, 256:384], rsc, add))
        need("v", t_tt)
        t_t = done("v", V.tensor_scalar(tt, tt0, imf, None, add))
        need("v", t)
        t = done("v", V.tensor_scalar(rs, rp, (-1.0, 2048.0)[q], None, add))
        need("v", t)
        t = done("v", V.tensor_scalar(ra, rs, 127, None, AluOpType.bitwise_and))
        tb = done("v", V.tensor_scalar(rb, rs, 7, None, AluOpType.arith_shift_right))
        need("v", t)
        t = done("v", V.tensor_scalar(rc, ra, 16.0, 2048.0, mult, add))
        need("v", t, tb)
        t = done("v", V.tensor_tensor(rd, rc, rb, add))
        need("v", t, t_t)
        t = done("v", V.tensor_tensor(rf, rd, tt, sub))
        need("v", t, t_k)
        t = done("v", V.tensor_tensor(rg, rk, rf, mult))
        need("v", t)
        t = done("v", V.tensor_tensor(rh, rg, tt, add))
        need("v", t)
        t_ro = done("v", V.tensor_copy(T.ro[:, :], rh))

    fs = [2 * k + i for k in order for i in range(2)]
    H0, H1, P0, P1 = range(4)
    ready = t_xm + t_xf
    units = [(f, H0) for f in fs[0:2]] + [(f, H1) for f in fs[0:2]] + [(f, H0) for f in fs[2:]] + \
            [(f, P0) for f in fs] + [(f, P1) for f in fs] + [(f, H1) for f in fs[2:]]
    U = len(units)
    t_hr, t_l2 = [None] * U, [None] * U
    first, last = {}, {}
    for u, (f, s) in enumerate(units):
        first.setdefault(s, u)
        last[s] = u
    near = [r for r in ranks if r != core]
    t_yp = [expect("yp%d" % j, len(engines([core], partner))) for j in range(2)]
    t_sc = [expect("sc%d" % j, len(engines([core], across))) for j in range(2)]
    t_sa, t_y = [None, None], [None, None]

    def give(j):
        need("v", t_l2[last[P0 + j]])
        t = done("v", V.tensor_copy(T.yo[:, chunk(j)], T["yb%d" % (P0 + j)][:, 0:Q]))
        need("g", t)
        send([([partner], T.yo[:, chunk(j)], T.yp[:, chunk(j)], "yp%d" % j)], 1)

    def cross(j):
        need("v", t_l2[last[j]], t_yp[j])
        t_sa[j] = done("v", V.tensor_tensor(T.sa[:, chunk(j)], T["yb%d" % j][:, 0:Q], T.yp[:, chunk(j)], add))
        need("g", t_sa[j])
        send([([across], T.sa[:, chunk(j)], T.sc[:, chunk(j)], "sc%d" % j)], 1)

    def deliver(j):
        j0 = RES + 1024 * d + off_w + Q * j
        dst = T.xr[:, j0:j0 + Q]
        src = dst if is_rank else T.ys[:, chunk(j)]
        need("v", t_sa[j], t_sc[j])
        t_y[j] = done("v", V.tensor_tensor(src, T.sa[:, chunk(j)], T.sc[:, chunk(j)], add))
        need("g", t_y[j])
        send([(near, src, dst, "res")], 1)

    for step in range(U + LOOK):
        if step < U:
            u = step
            f, s = units[u]
            hb, hr = T["hb%d" % (u % NH)], T["hr%d" % (u % NR)]
            need("pe", hb_free[u % NH], piece[0][f // 2], ready[s])
            t = done("pe", PE.matmul(hb[:, 0:Q], T.wa[:, 128 * f:128 * f + 128], T.xx[:, Q * s:Q * s + Q], True, True))
            need("s", t, t_l2[u - NR] if u >= NR else None)
            t_hr[u] = hb_free[u % NH] = done("s", S.activation(hr[:, 0:Q], hb[:, 0:Q], Relu))
        if step >= LOOK:
            u = step - LOOK
            f, s = units[u]
            hr = T["hr%d" % (u % NR)]
            need("pe", t_hr[u], piece[1][f // 2])
            m = PE.matmul(T["yb%d" % s][:, 0:Q], T.wb[:, 128 * f:128 * f + 128], hr[:, 0:Q], u == first[s], u == last[s])
            t_l2[u] = done("pe", m)
            if u == last[P0]:
                give(0)
                cross(0)
            if u == last[P1]:
                give(1)
    cross(1)
    deliver(0)
    deliver(1)

    if is_rank:
        n = sum(2 * len(engines([core], c)) for tm in teams[q] for c in tm if c != core)
        t_res = expect("res", n)
        need("v", t_res, t_ro, *t_y)
        need("s", t_res, t_ro, *t_y)
        for i in range(2):
            cv, cs = slice(512 * i, 512 * i + 512), slice(1024 + 512 * i, 1536 + 512 * i)
            tv = done("v", V.tensor_copy(T.yt[:, cv], T.xr[:, 4:4100].indirect(T.ro[:, 32 * i:32 * i + 32])))
            ts = done("s", S.activation(T.yt[:, cs], T.xr[:, 4:4100].indirect(T.ro[:, 64 + 32 * i:96 + 32 * i]), Copy))
            need("sy", tv)
            dma(g.sync.dma_start(T.y[:, cv], T.yt[:, cv]), "d_st")
            qn = ("sy", "s")[i]
            need(qn, ts)
            dma(queues[qn].dma_start(T.y[:, cs], T.yt[:, cs]), "d_st")
    for s in sorted(total):
        if seen.get(s, 0) < total[s]:
            need("g", (s, total[s]))
